import numpy as np, ml_dtypes
CORES = [83,85,87,115,117,119]
N = 6
import mx_ref
BF = ml_dtypes.bfloat16
def entries(a):
    return np.ascontiguousarray(a.T).reshape(-1)
def table(e):
    return np.ascontiguousarray(np.reshape(e, (-1, 16)).T).astype(np.int32)
def gpick(z, e):
    return np.concatenate([z[16 * g:16 * g + 16][:, e[g]] for g in range(8)])
def tile(rs):
    return np.stack(rs, axis=2).reshape(128, -1).astype(BF)
def cut(t, i, w=512):
    return t[:, w * i:w * i + w]
def f(rng, *shape):
    return mx_ref.flush((rng.standard_normal(shape, dtype=np.float32) * np.exp2(rng.integers(-2, 3, shape[:-1] + (1,)))).astype(BF))
def wide(rng, *shape, cols=0):
    v = rng.standard_normal(shape, dtype=np.float32) * np.exp2(rng.integers(-12, 13, shape)).astype(np.float32)
    if cols: v *= np.repeat(np.exp2(rng.integers(-cols, cols + 1, shape[:-2] + (1, shape[-1] // 4))) * (rng.random(shape[:-2] + (1, shape[-1] // 4)) > 0.0625), 4, axis=-1).astype(np.float32)
    return mx_ref.flush(v.astype(BF))
TQ, O = 256, 1
def lay(k, q):
    return {"kp": np.repeat(k, 16, axis=1).astype(np.int32), "qp": np.stack([table(e) for e in q])}
def setup_inputs(rng):
    d = {"qx": f(rng, N, 128, 4 * TQ), "ky": f(rng, N, 128, 2048), "rt": np.repeat(f(rng, 1, 128, 1024), N, axis=0), "vv": f(rng, N, 128, 512 * O)}
    a = rng.integers(0, 3585)
    k = a + rng.integers(0, 512, (N, 8, 4))
    q = np.where(rng.random((N, TQ)) < 0.25, rng.integers(0, 4096, (N, TQ)), a + rng.integers(0, 512, (N, TQ)))
    return {**d, **lay(k, q)}
def setup_inputs_far(rng):
    d = setup_inputs(rng)
    k = rng.integers(1500, 2501, (N, 32)); q = np.zeros((N, TQ), int); a = int(rng.integers(0, 2))
    for r in range(N):
        k[r, rng.permutation(32)[:2]] = [1500, 2500]
        lo, hi = (2628, 4095) if (r + a) % 2 else (0, 1371)
        q[r] = rng.integers(lo, hi + 1, TQ)
        q[r, rng.permutation(TQ)[:2]] = [lo, hi]
    return {**d, **lay(k.reshape(N, 8, 4), q)}
def setup_inputs_same(rng):
    d = setup_inputs(rng); a = int(rng.integers(0, 4096))
    return {**d, **lay(np.full((N, 8, 4), a), np.full((N, TQ), a))}
def setup_inputs_descending(rng):
    d = setup_inputs(rng); a = rng.integers(0, 3585)
    q = np.stack([a + np.sort(rng.permutation(512)[:TQ])[::-1] for r in range(N)])
    k = np.stack([a + 16 * rng.permutation(32) + rng.integers(0, 16, 32) for r in range(N)])
    return {**d, **lay(k.reshape(N, 8, 4), q)}
def setup_inputs_near(rng):
    d = setup_inputs(rng); a = rng.integers(2049, 3968)
    q = np.stack([a + rng.permutation(TQ) % 128 for r in range(N)])
    k = np.stack([a + rng.permutation(np.concatenate([[0, 128], 1 + rng.permutation(127)[:30]])) for r in range(N)])
    return {**d, **lay(k.reshape(N, 8, 4), q)}
def setup_inputs_spread(rng):
    d = setup_inputs(rng); d["qx"] = wide(rng, N, 128, 4 * TQ, cols=4); return d
def check_inputs(d):
    b = []
    for r in range(N):
        k, q = d["kp"][r], entries(d["qp"][r])
        if d["rt"][r].tobytes() != d["rt"][0].tobytes(): b.append("rt")
        if k.min() < 0 or k.max() > 4095 or (k != np.repeat(k[::16], 16, axis=0)).any(): b.append("kp")
        if q.min() < 0 or q.max() > 4095: b.append("qp")
    return b
def reference(qx, ky, rt, vv, kp, qp):
    y = np.zeros((N, 128, O * TQ), np.float32)
    X = [mx_ref.quantize(qx[r]) for r in range(N)]
    for s in range(N):
        K = [mx_ref.quantize(np.ascontiguousarray(cut(ky[s], b))) for b in range(4)]
        V = [mx_ref.quantize(np.ascontiguousarray(cut(vv[s], o))) for o in range(O)]
        R = mx_ref.quantize(rt[s])
        P = [mx_ref.matmul(K[b], R) for b in range(4)]
        for r in range(N):
            A = []
            for b in range(4):
                c = np.clip(entries(qp[r])[None, :] - kp[s][::16, b][:, None], -128, 127) + 128
                A.append(np.maximum(mx_ref.matmul(K[b], X[r]) + gpick(P[b], c), np.float32(0)) * np.float32(0.03125))
            A = mx_ref.quantize(tile(A))
            for o in range(O): y[r][:, TQ * o:TQ * o + TQ] += mx_ref.matmul(V[o], A)
    return {"y": y}

@@ -1,0 +1,315 @@
+from concourse.bass import DstId, RemoteDMATransfer
+from concourse.mybir import dt, AluOpType, ActivationFunctionType
+
+NR, TQ = 6, 256
+F8 = "float8_e4m3fn_x4"
+RT, OWN, PRV, NXT = 0, 256, 512, 768
+SCRATCH = {
+    "kt": ("sbuf", [128, 2048], "bfloat16"),
+    "xt": ("sbuf", [128, 1024], "bfloat16"),
+    "rtt": ("sbuf", [128, 1024], "bfloat16"),
+    "vt": ("sbuf", [128, 512], "bfloat16"),
+    "mc": ("sbuf", [128, 1024], F8), "mp": ("sbuf", [128, 1024], "uint8"),
+    "kco": ("sbuf", [128, 512], F8), "kpo": ("sbuf", [128, 512], "uint8"),
+    "kcf": ("sbuf", [128, 512], F8), "kpf": ("sbuf", [128, 512], "uint8"),
+    "kpi": ("sbuf", [128, 4], "int32"),
+    "kfo": ("sbuf", [128, 4], "float32"), "kff": ("sbuf", [128, 4], "float32"),
+    "qpi": ("sbuf", [128, 48], "int32"),
+    "pwo": ("sbuf", [128, 1024], "float32"), "pwf": ("sbuf", [128, 1024], "float32"),
+    "ys": ("sbuf", [128, 256], "float32"),
+}
+for _n, _w in (("o", 64), ("x", 128), ("f", 64)):
+    SCRATCH["ot" + _n] = ("sbuf", [128, _w], "float32")
+    SCRATCH["of" + _n] = ("sbuf", [128, _w], "uint16")
+for _i in range(4):
+    SCRATCH["gg%d" % _i] = ("sbuf", [128, 1024], "float32")
+    SCRATCH["ht%d" % _i] = ("sbuf", [128, 1024], "bfloat16")
+for _i in range(2):
+    SCRATCH["oc%d" % _i] = ("sbuf", [128, TQ], F8)
+    SCRATCH["op%d" % _i] = ("sbuf", [128, TQ], "uint8")
+for _i in range(NR):
+    SCRATCH["vc%d" % _i] = ("sbuf", [128, 128], F8)
+    SCRATCH["vp%d" % _i] = ("sbuf", [128, 128], "uint8")
+    SCRATCH["ac%d" % _i] = ("sbuf", [128, TQ], F8)
+    SCRATCH["ap%d" % _i] = ("sbuf", [128, TQ], "uint8")
+for _i in range(8):
+    SCRATCH["ps%d" % _i] = ("psum", [128, 512], "float32")
+
+SEMAPHORES = (["l_p", "l_q", "l_k0", "l_k1", "l_v", "l_r", "l_x", "vs", "ss", "ts", "sent", "stored",
+               "q_in", "kf_in", "k0_in", "k1_in", "r_in", "xp_in", "xn_in"]
+              + ["%s_in%d" % (n, i) for n in ("v", "a") for i in range(NR)])
+
+
+def layout(T, topo):
+    cores = list(T.cores)
+    side = [[q for q in range(NR) if topo.chip(cores[q]) == topo.chip(cores[r])] for r in range(NR)]
+    local, mirror, worker = [], [], []
+    for r in range(NR):
+        i = side[r].index(r)
+        local.append(side[r][i:] + side[r][:i])
+        mirror.append([q for q in range(NR) if q not in side[r]][i])
+    for r in range(NR):
+        idle = [c for c in topo.cores_of(cores[r]) if c not in cores and c not in worker]
+        idle.sort(key=lambda c: (topo.die(c) != topo.die(cores[mirror[r]]), -c))
+        worker.append(idle[0])
+    return cores, local, mirror, worker
+
+
+def rank_program(g, core, T, topo):
+    cores, local, mirror, worker = layout(T, topo)
+    rank = T.rank_of(core)
+    if rank is None and core not in worker:
+        return
+    r, nxt, prv = local[rank if rank is not None else worker.index(core)]
+    far_s = mirror[r]
+    ADD, MAX, MIN, MULT, SUB = AluOpType.add, AluOpType.max, AluOpType.min, AluOpType.mult, AluOpType.subtract
+    COPY = ActivationFunctionType.Copy
+    eng = {"g": g, "v": g.vector, "s": g.scalar, "t": g.tensor}
+    done, seen, sent = {"v": 0, "s": 0, "t": 0}, {}, [0]
+
+    def after(q, *deps):
+        for d in deps:
+            sem = d[0] + "s" if d[0] in done else d[0]
+            if seen.get((q, sem), 0) < d[1]:
+                eng[q].wait_ge(T.sem[sem], d[1])
+                seen[(q, sem)] = d[1]
+
+    def mark(q, ins):
+        ins.then_inc(T.sem[q + "s"], 1)
+        done[q] += 1
+        return (q, done[q])
+
+    far = cores[mirror[0]] if topo.chip(core) == topo.chip(cores[0]) else cores[0]
+    near = [c for c in topo.cores_of(core) if c != core][0]
+    ALL = topo.engines(core, near)
+    OFF = topo.engines(core, far)
+    ON = [e for e in ALL if e not in OFF]
+    nALL, nOFF, nON = len(ALL), len(OFF), len(ON)
+
+    def ids(dsts):
+        out = []
+        for d in dsts:
+            rid, pid = topo.addr(d)[:2]
+            out.append(DstId(rid=rid, pnc=pid))
+        return out
+
+    def send(sems, src, *ways):
+        if not isinstance(sems, list):
+            sems = [sems] * len(ways)
+        g.remote_dma_fused([RemoteDMATransfer(dst_ids=ids(ds), dma_engine_mask=sum(1 << e for e in es), remote_sem=T.sem[sem],
+                                              srcs=[src], dsts=[to] * len(ds)) for sem, (es, ds, to) in zip(sems, ways)], local_sem=T.sem.sent)
+        sent[0] += sum(len(es) for es, _, _ in ways)
+
+    def codes(name, a, b):
+        return T[name][:, a:b].bitcast(dt.uint8)
+
+    def plane(name, a, b):
+        return T[name][:, a:b]
+
+    def ship(sems, src, a, n, *ways):
+        for k, view in ((0, codes), (1, plane)):
+            send(sems, view(src[k], a, a + n), *[(es, ds, view(to[k], ta, ta + n)) for es, ds, to, ta in ways])
+
+    M, KO, KF = ("mc", "mp"), ("kco", "kpo"), ("kcf", "kpf")
+
+    def V(s):
+        return ("vc%d" % s, "vp%d" % s)
+
+    def A(s):
+        return ("ac%d" % s, "ap%d" % s)
+
+    def quantise(to, a, b, src, *deps):
+        after("v", *deps)
+        return mark("v", g.vector.quantize_mx(T[to[0]][:, a:b], T[to[1]][:, a:b], src))
+
+    def lists(n, kf, a, w, *deps):
+        after("v", *deps)
+        for b in range(4):
+            m = mark("v", g.vector.tensor_scalar(T["ot" + n][:, w * b:w * b + w], T.qpi[:, a:a + w], T[kf][:, b:b + 1], 0.0, SUB, MAX))
+        after("v", m)
+        return mark("v", g.vector.tensor_scalar(T["of" + n][:], T["ot" + n][:], 255.0, None, MIN))
+
+    banks = 7 if rank is not None else 8
+    drained, turn = [()] * 8, [0]
+    P, W, S, G, R = {}, {}, {}, {}, {}
+
+    def product(K, b, a):
+        k = turn[0] % banks
+        turn[0] += 1
+        after("t", *drained[k])
+        return k, mark("t", g.tensor.matmul_mx(T["ps%d" % k][:, 0:TQ], T[K[0]][:, 128 * b:128 * b + 128], T[K[1]][:, 128 * b:128 * b + 128],
+                                               T.mc[:, a:a + TQ], T.mp[:, a:a + TQ], True, True))
+
+    def distances(n, K, bs, *deps):
+        after("t", *deps)
+        for b in bs:
+            P[n, b] = product(K, b, RT)
+
+    def scores(i, K, a, *deps):
+        after("t", *deps)
+        for b in range(4):
+            S[i, b] = product(K, b, a)
+
+    def window(n, b, q):
+        k, m = P[n, b]
+        d, p = T["pw" + n][:, TQ * b:TQ * b + TQ], T["ps%d" % k][:, 0:TQ]
+        after(q, m)
+        W[n, b] = mark(q, g.vector.tensor_copy(d, p) if q == "v" else g.scalar.activation(d, p, COPY))
+        drained[k] = (W[n, b],)
+
+    def pick(i, n, b, of, col, li):
+        after("s", W[n, b], li)
+        G[i, b] = mark("s", g.scalar.activation(T["gg%d" % i][:, TQ * b:TQ * b + TQ],
+                                                T["pw" + n][:, TQ * b:TQ * b + TQ].indirect(T[of][:, col:col + 16]), COPY))
+
+    def add(i, b):
+        k, m = S[i, b]
+        after("v", m, G[i, b])
+        R[i, b] = mark("v", g.vector.tensor_tensor(T["ht%d" % i][:, b:4 * TQ:4], T["ps%d" % k][:, 0:TQ], T["gg%d" % i][:, TQ * b:TQ * b + TQ], ADD))
+        drained[k] = (R[i, b],)
+
+    def relu(i, b, step):
+        after("v", *[R[i, c] for c in range(b, 4, step)])
+        h = T["ht%d" % i][:, b:4 * TQ:step]
+        R[i] = mark("v", g.vector.tensor_scalar(h, h, 0.0, 0.03125, MAX, MULT))
+
+    def pack(i, to):
+        return quantise(to, 0, TQ, T["ht%d" % i][:], R[i])
+
+    def lace(i, j, to):
+        add(j, 0)
+        relu(i, 0, 1)
+        add(j, 1)
+        m = pack(i, to)
+        add(j, 2)
+        return m
+
+    def close(i, to):
+        relu(i, 0, 2)
+        add(i, 3)
+        relu(i, 1, 2)
+        return pack(i, to)
+
+    def farewell():
+        after("g", ("v", done["v"]), ("s", done["s"]), ("t", done["t"]), ("sent", sent[0]))
+
+    B = range(4)
+    QIN = ("q_in", nON + nOFF)
+    if rank is None:
+        here, home = [cores[r]], [cores[q] for q in local[r]]
+        KFIN = ("kf_in", nOFF)
+        after("g", KFIN)
+        send("kf_in", T.kff[:], (ALL, here, T.kff[:]))
+        for i in range(2):
+            after("g", ("k%d_in" % i, 2 * nOFF))
+            ship("k%d_in" % i, KF, 256 * i, 256, (ALL, here, KF, 256 * i))
+        after("g", ("v_in%d" % far_s, 2 * nOFF))
+        ship("v_in%d" % far_s, V(far_s), 0, 128, (ALL, home, V(far_s), 0))
+
+        li = lists("x", "kff", 16, 32, QIN, KFIN)
+        distances("f", KF, (0, 1), ("r_in", 2 * nON), ("k0_in", 2 * nOFF))
+        distances("f", KF, (2, 3), ("k1_in", 2 * nOFF))
+        window("f", 0, "s")
+        for b in (1, 2, 3):
+            window("f", b, "v")
+        for i in range(2):
+            for b in B:
+                pick(i, "f", b, "ofx", 32 * b + 16 * i, li)
+        scores(0, KF, PRV, ("xp_in", 2 * nON))
+        for b in B:
+            add(0, b)
+        scores(1, KF, NXT, ("xn_in", 2 * nOFF))
+        made = [lace(0, 1, ("oc0", "op0")), close(1, ("oc1", "op1"))]
+        for i, q in ((0, prv), (1, nxt)):
+            after("g", made[i])
+            ship("a_in%d" % far_s, ("oc%d" % i, "op%d" % i), 0, TQ, (ALL, [cores[q]], A(far_s), 0))
+        farewell()
+        return
+
+    away, mine = [worker[far_s]], [worker[r]]
+    to_nxt, to_prv = [cores[nxt], worker[nxt]], [cores[prv], worker[prv]]
+    g.sync.dma_start(T.kpi[:], T.kp[:]).then_inc(T.sem.l_p, 16)
+    for i in range(2):
+        g.sync.dma_start(T.kt[:, 1024 * i:1024 * i + 1024], T.ky[:, 1024 * i:1024 * i + 1024]).then_inc(T.sem["l_k%d" % i], 16)
+    g.sync.dma_start(T.rtt[:], T.rt[:]).then_inc(T.sem.l_r, 16)
+    for k in range(8):
+        g.scalar.dma_start(T.qpi[16 * k:16 * k + 16, 0:16], T.qp[:]).then_inc(T.sem.l_q, 16)
+    g.scalar.dma_start(T.xt[:], T.qx[:]).then_inc(T.sem.l_x, 16)
+    g.scalar.dma_start(T.vt[:], T.vv[:]).then_inc(T.sem.l_v, 16)
+    LQ = ("l_q", 16 * 8)
+
+    after("v", ("l_p", 16))
+    mf = mark("v", g.vector.tensor_scalar(T.kfo[:], T.kpi[:], 128.0, None, SUB))
+    after("g", mf)
+    send("kf_in", T.kfo[:], (OFF, away, T.kff[:]))
+    after("g", LQ)
+    send("q_in", T.qpi[:, 0:16], (ON, to_nxt, T.qpi[:, 16:32]), (OFF, to_prv, T.qpi[:, 32:48]))
+    for i in range(2):
+        mk = quantise(KO, 256 * i, 256 * i + 256, T.kt[:, 1024 * i:1024 * i + 1024], ("l_k%d" % i, 16))
+        after("g", mk)
+        ship("k%d_in" % i, KO, 256 * i, 256, (OFF, away, KF, 256 * i))
+    lo = lists("o", "kfo", 0, 16, mf, LQ)
+    mr = quantise(M, RT, RT + TQ, T.rtt[:], ("l_r", 16))
+    after("g", mr)
+    ship("r_in", M, RT, TQ, (ON, mine, M, RT))
+    mx = quantise(M, OWN, OWN + TQ, T.xt[:], ("l_x", 16))
+    after("g", mx)
+    ship(["xp_in", "xn_in"], M, OWN, TQ, (ON, to_nxt, M, PRV), (OFF, to_prv, M, NXT))
+
+    distances("o", KO, B, mk, mr)
+    for b, q in ((0, "s"), (1, "s"), (2, "v"), (3, "v")):
+        window("o", b, q)
+    scores(0, KO, OWN, mx)
+    for b in B:
+        pick(0, "o", b, "ofo", 16 * b, lo)
+    add(0, 0)
+    lx = lists("x", "kfo", 16, 32, QIN)
+    for i in range(2):
+        for b in B:
+            pick(1 + i, "o", b, "ofx", 32 * b + 16 * i, lx)
+    add(0, 1)
+    mv = quantise(V(r), 0, 128, T.vt[:], ("l_v", 16))
+    after("g", mv)
+    ship("v_in%d" % r, V(r), 0, 128, (OFF, away, V(r), 0), (ON, [cores[nxt], cores[prv]], V(r), 0))
+    add(0, 2)
+    add(0, 3)
+    scores(1, KO, PRV, ("xp_in", 2 * nON))
+    made = {r: lace(0, 1, A(r))}
+    lf = lists("f", "kff", 0, 16, ("kf_in", nALL))
+    add(1, 3)
+    scores(2, KO, NXT, ("xn_in", 2 * nOFF))
+    m1 = lace(1, 2, ("oc0", "op0"))
+    add(2, 3)
+    relu(2, 0, 1)
+    m2 = pack(2, ("oc1", "op1"))
+    for i, q, m in ((0, prv, m1), (1, nxt, m2)):
+        after("g", m)
+        ship("a_in%d" % r, ("oc%d" % i, "op%d" % i), 0, TQ, (ALL, [cores[q]], A(r), 0))
+
+    order = [r, nxt, prv, mirror[nxt], far_s, mirror[prv]]
+
+    def value(s):
+        after("t", mv if s == r else ("v_in%d" % s, 2 * (nON if s in (prv, nxt) else nALL)))
+        after("t", made[s] if s in made else ("a_in%d" % s, 2 * nALL))
+        return mark("t", g.tensor.matmul_mx(T.ps7[:, 0:TQ], T["vc%d" % s][:], T["vp%d" % s][:], T["ac%d" % s][:], T["ap%d" % s][:],
+                                            s == order[0], s == order[-1]))
+
+    value(r)
+    distances("f", KF, (0, 1), ("k0_in", 2 * nALL))
+    distances("f", KF, (2, 3), ("k1_in", 2 * nALL))
+    for b, q in ((0, "s"), (1, "s"), (2, "v"), (3, "v")):
+        window("f", b, q)
+    for b in B:
+        pick(3, "f", b, "off", 16 * b, lf)
+    scores(3, KF, OWN)
+    for b in range(3):
+        add(3, b)
+    made[far_s] = close(3, A(far_s))
+    for s in order[1:]:
+        m = value(s)
+    after("s", m)
+    m = mark("s", g.scalar.activation(T.ys[:], T.ps7[:, 0:TQ], COPY))
+    after("s", m)
+    g.scalar.dma_start(T.y[:], T.ys[:]).then_inc(T.sem.stored, 16)
+    after("g", ("stored", 16))
+    farewell()

@@ -1,315 +1,324 @@
 from concourse.bass import DstId, RemoteDMATransfer
 from concourse.mybir import dt, AluOpType, ActivationFunctionType
 
-NR, TQ = 6, 256
+NR, TQ, U = 6, 256, 128
 F8 = "float8_e4m3fn_x4"
-RT, OWN, PRV, NXT = 0, 256, 512, 768
 SCRATCH = {
     "kt": ("sbuf", [128, 2048], "bfloat16"),
     "xt": ("sbuf", [128, 1024], "bfloat16"),
     "rtt": ("sbuf", [128, 1024], "bfloat16"),
     "vt": ("sbuf", [128, 512], "bfloat16"),
-    "mc": ("sbuf", [128, 1024], F8), "mp": ("sbuf", [128, 1024], "uint8"),
-    "kco": ("sbuf", [128, 512], F8), "kpo": ("sbuf", [128, 512], "uint8"),
-    "kcf": ("sbuf", [128, 512], F8), "kpf": ("sbuf", [128, 512], "uint8"),
-    "kpi": ("sbuf", [128, 4], "int32"),
-    "kfo": ("sbuf", [128, 4], "float32"), "kff": ("sbuf", [128, 4], "float32"),
+    "rc": ("sbuf", [128, TQ], F8), "rp": ("sbuf", [128, TQ], "uint8"),
+    "xc": ("sbuf", [128, 3 * TQ], F8), "xp": ("sbuf", [128, 3 * TQ], "uint8"),
+    "kc": ("sbuf", [128, 1024], F8), "ks": ("sbuf", [128, 1024], "uint8"),
+    "kpi": ("sbuf", [128, 8], "int32"), "kf": ("sbuf", [128, 8], "float32"),
     "qpi": ("sbuf", [128, 48], "int32"),
-    "pwo": ("sbuf", [128, 1024], "float32"), "pwf": ("sbuf", [128, 1024], "float32"),
-    "ys": ("sbuf", [128, 256], "float32"),
+    "of": ("sbuf", [128, 8 * 48], "uint16"),
+    "pw": ("sbuf", [128, 8 * TQ], "float32"),
+    "gg": ("sbuf", [128, 24 * TQ], "float32"),
+    "ht": ("sbuf", [128, 24 * TQ], "bfloat16"),
+    "oc": ("sbuf", [128, 3 * TQ], F8), "op": ("sbuf", [128, 3 * TQ], "uint8"),
+    "vc": ("sbuf", [128, NR * 128], F8), "vp": ("sbuf", [128, NR * 128], "uint8"),
+    "ac": ("sbuf", [128, NR * TQ], F8), "ap": ("sbuf", [128, NR * TQ], "uint8"),
+    "ys": ("sbuf", [128, TQ], "float32"),
 }
-for _n, _w in (("o", 64), ("x", 128), ("f", 64)):
-    SCRATCH["ot" + _n] = ("sbuf", [128, _w], "float32")
-    SCRATCH["of" + _n] = ("sbuf", [128, _w], "uint16")
-for _i in range(4):
-    SCRATCH["gg%d" % _i] = ("sbuf", [128, 1024], "float32")
-    SCRATCH["ht%d" % _i] = ("sbuf", [128, 1024], "bfloat16")
-for _i in range(2):
-    SCRATCH["oc%d" % _i] = ("sbuf", [128, TQ], F8)
-    SCRATCH["op%d" % _i] = ("sbuf", [128, TQ], "uint8")
-for _i in range(NR):
-    SCRATCH["vc%d" % _i] = ("sbuf", [128, 128], F8)
-    SCRATCH["vp%d" % _i] = ("sbuf", [128, 128], "uint8")
-    SCRATCH["ac%d" % _i] = ("sbuf", [128, TQ], F8)
-    SCRATCH["ap%d" % _i] = ("sbuf", [128, TQ], "uint8")
 for _i in range(8):
     SCRATCH["ps%d" % _i] = ("psum", [128, 512], "float32")
 
-SEMAPHORES = (["l_p", "l_q", "l_k0", "l_k1", "l_v", "l_r", "l_x", "vs", "ss", "ts", "sent", "stored",
-               "q_in", "kf_in", "k0_in", "k1_in", "r_in", "xp_in", "xn_in"]
-              + ["%s_in%d" % (n, i) for n in ("v", "a") for i in range(NR)])
+SEMAPHORES = (["l_p", "l_q", "l_v", "l_r", "l_x", "vs", "ss", "ts", "sent", "stored", "kp", "r"]
+              + ["%s%d" % (n, i) for n in ("kc", "ks", "kk", "l_k") for i in range(4)]
+              + ["%s%d" % (n, i) for n in "qx" for i in range(3)] + ["%s%d" % (n, i) for n in "va" for i in range(NR)])
+SPAN = {"p": (0, 2), "n": (2, 4), "i": (4, 6), "w": (0, 4), "z": (2, 6), "a": (0, 6),
+        "0": (0, 1), "1": (1, 2), "2": (2, 3), "3": (3, 4), "4": (4, 5), "5": (5, 6)}
+CFG = {
+    "loads": "k02 x r k24 v",
+    "rank.g": "kp OFF A; q ON Fn Cn Cp Fp; kk02 OFF A; x ON Fn; r ON Fi; x ON Cn; kk24 OFF A; x ON Fp / OFF Cp; v OFF A / ON Cn Cp; ap ALL Cp; an ALL Cn",
+    "first.g": "kp ALL Ci; kk02 ALL Ci; kk24 ALL Ci; v ALL C0 C1 C2; ap ALL Cp; an ALL Cn",
+    "rank.v": "C1 C2 C3 F0 Qk02 Li0 Qx Qr Qk24 Qv W2 W3 Ai0 Lw0 Ai1 Ai2 Ai3 Ri01 Zi0 Ap0 Ap1 Ap2 Ap3 F4 Rp01 Li4 Zp0 An0 An1 An2 An3 Rn01 Zn0 Ai4 Ai5 Ai6 Ai7 Ri64 Ri74 Zi4",
+    "rank.s": "W0 W1 Gi0 Gi1 Gi2 Gi3 Gp0 Gp1 Gp2 Gp3 Gn0 Gn1 Gn2 Gn3 W4 W5 Gi4 Gi5 W6 W7 Gi6 Gi7 Ri44 Ri54 O01",
+    "rank.t": "P0 P1 P2 P3 Si0 Si1 Si2 Si3 Sp0 Sp1 Sp2 Sp3 Sn0 Sn1 P4 P5 Sn2 Sn3 Si4 Si5 P6 P7 Si6 Si7",
+    "rank.y": "Ci Cn Fn Cp Fi Fp",
+    "first.v": "F0 Lw0 W1 Ap0 Ap1 An0 Rw04 An1 W3 Rw14 Ap2 Rp24 Ap3 Rp34 Zp0 An2 An3 Rn24 Rn34 Zn0",
+    "first.s": "W0 Gp0 Gp1 Gn0 Gn1 W2 Gp2 Gp3 Gn2 Gn3",
+    "first.t": "P0 P1 Sp0 Sp1 Sn0 Sn1 P2 P3 Sp2 Sp3 Sn2 Sn3",
+}
 
 
 def layout(T, topo):
     cores = list(T.cores)
-    side = [[q for q in range(NR) if topo.chip(cores[q]) == topo.chip(cores[r])] for r in range(NR)]
-    local, mirror, worker = [], [], []
-    for r in range(NR):
-        i = side[r].index(r)
-        local.append(side[r][i:] + side[r][:i])
-        mirror.append([q for q in range(NR) if q not in side[r]][i])
-    for r in range(NR):
-        idle = [c for c in topo.cores_of(cores[r]) if c not in cores and c not in worker]
-        idle.sort(key=lambda c: (topo.die(c) != topo.die(cores[mirror[r]]), -c))
-        worker.append(idle[0])
-    return cores, local, mirror, worker
+    sides = []
+    for chip in sorted({topo.chip(c) for c in cores}):
+        ranks = [q for q in range(NR) if topo.chip(cores[q]) == chip]
+        ranks.sort(key=lambda q: sum(topo.die(cores[p]) == topo.die(cores[q]) for p in ranks))
+        sides.append(ranks)
+    first, second = {}, {}
+    for k in range(2):
+        idle = [c for c in topo.cores_of(cores[sides[k][0]]) if c not in cores]
+        for s in sides[1 - k]:
+            idle.sort(key=lambda c: (topo.die(c) != topo.die(cores[s]), -c))
+            first[s] = idle.pop(0)
+        for s in sides[1 - k][1:]:
+            second[s] = idle.pop(0)
+    return cores, sides, first, second
+
+
+def plan(T, topo):
+    cores, sides, first, second = layout(T, topo)
+    ALL = topo.engines(cores[sides[0][0]], cores[sides[0][1]])
+    OFF = topo.engines(cores[sides[0][0]], cores[sides[1][0]])
+    ON = [e for e in ALL if e not in OFF]
+    h = len(OFF) // 2
+    E = {"ALL": ALL, "OFF": OFF, "ON": ON, "LO": OFF[:h], "HI": OFF[h:], "EV": OFF[::2], "OD": OFF[1::2], "ON1": ON[:h], "ON2": ON[h:]}
+    calls, role = {}, {}
+    for k in range(2):
+        home, far = sides[k], sides[1 - k]
+        for i, r in enumerate(home):
+            at = {"i": i, "n": (i + 1) % 3, "p": (i + 2) % 3, "0": 0, "1": 1, "2": 2}
+            who = {"A": first[r]}
+            for a, j in at.items():
+                who["C" + a], who["F" + a], who["X" + a] = cores[home[j]], first[far[j]], second.get(far[j])
+                who["A" + a], who["B" + a], who["M" + a] = first[home[j]], second.get(home[j]), cores[far[j]]
+            for kind, c, keys in (("rank", who["Ci"], r), ("first", who["Fi"], far[i]), ("second", who["Xi"], far[i])):
+                text = CFG.get("%s%d.g" % (kind, i), CFG.get(kind + ".g"))
+                if c is None or text is None:
+                    continue
+                me = i
+                if kind == "second":
+                    w = CFG.get("second%d.keys" % i, "Fi")
+                    keys, me = (home if w[0] == "C" else far)[at[w[1]]], at[w[1]]
+                role[c] = (kind, keys, me, home, far, i)
+                calls[c] = []
+                for text in text.split(";"):
+                    name, rest = text.split(None, 1)
+                    ways = [(E[w.split()[0]], [who[d] for d in w.split()[1:]]) for w in rest.split("/")]
+                    if name[0] in "qx":
+                        piece = (name[0], at[name[1:] or "i"])
+                    elif name[0] == "a":
+                        piece = ("a", keys) + SPAN[name[1]]
+                    elif name[0] == "v":
+                        piece = ("v", keys if name == "v" else (home if name[1] == "C" else far)[at[name[2]]])
+                    else:
+                        piece = (name,)
+                    calls[c].append((piece, ways))
+    return cores, calls, role
+
+
+def slot(i, me):
+    return 2 - (i - me) % 3
+
+
+def pieces(piece, me, there):
+    n, later, there = piece[0], there[0] == "rank", there[2]
+    if n == "kp":
+        return "kp", [("kpi", "kpi", 0, 4 * later, 4)]
+    if n == "q":
+        return "q%d" % piece[1], [("qpi", "qpi", 16 * slot(piece[1], me), 16 * slot(piece[1], there), 16)]
+    if n[:2] in ("kc", "ks", "kk"):
+        a, e = 128 * int(n[2]), 128 * int(n[3])
+        return n[:3], [(b, b, a, a + 512 * later, e - a) for b in (("kc", "ks") if n[1] == "k" else (n[:2],))]
+    if n == "r":
+        return "r", [("rc", "rc", 0, 0, TQ), ("rp", "rp", 0, 0, TQ)]
+    if n == "x":
+        return "x%d" % piece[1], [(b, b, TQ * slot(piece[1], me), TQ * slot(piece[1], there), TQ) for b in ("xc", "xp")]
+    if n == "v":
+        return "v%d" % piece[1], [(b, b, 128 * piece[1], 128 * piece[1], 128) for b in ("vc", "vp")]
+    s, u0, u1 = piece[1:]
+    return "a%d" % s, [(a, b, U * u0, TQ * s + U * (u0 % 2), U * (u1 - u0)) for a, b in (("oc", "ac"), ("op", "ap"))]
 
 
 def rank_program(g, core, T, topo):
-    cores, local, mirror, worker = layout(T, topo)
-    rank = T.rank_of(core)
-    if rank is None and core not in worker:
+    cores, calls, role = plan(T, topo)
+    if core not in role:
         return
-    r, nxt, prv = local[rank if rank is not None else worker.index(core)]
-    far_s = mirror[r]
+    kind, keys, me, home, far, idx = role[core]
+    place = [(me + 2) % 3, (me + 1) % 3, me]
+    due, block = {}, {}
+    for c in calls:
+        for piece, ways in calls[c]:
+            sem, parts = pieces(piece, 0, role[core])
+            for es, ds in ways:
+                if core in ds:
+                    due[sem] = due.get(sem, 0) + len(es) * len(parts)
+                    for a, _, _, ca, w in parts:
+                        if a in ("kc", "ks"):
+                            for b in range(ca // 128, (ca + w) // 128):
+                                block[a, b] = [sem]
     ADD, MAX, MIN, MULT, SUB = AluOpType.add, AluOpType.max, AluOpType.min, AluOpType.mult, AluOpType.subtract
-    COPY = ActivationFunctionType.Copy
-    eng = {"g": g, "v": g.vector, "s": g.scalar, "t": g.tensor}
-    done, seen, sent = {"v": 0, "s": 0, "t": 0}, {}, [0]
+    COPY, RELU = ActivationFunctionType.Copy, ActivationFunctionType.Relu
+    eng = {"g": g, "v": g.vector, "s": g.scalar, "t": g.tensor, "y": g.sync}
+    count, seen, sent = {"v": 0, "s": 0, "t": 0}, {}, [0]
+    at = {sem: (sem, due[sem]) for sem in due}
+    rank = kind == "rank"
 
-    def after(q, *deps):
+    def after(q, deps):
         for d in deps:
-            sem = d[0] + "s" if d[0] in done else d[0]
-            if seen.get((q, sem), 0) < d[1]:
-                eng[q].wait_ge(T.sem[sem], d[1])
-                seen[(q, sem)] = d[1]
+            if seen.get((q, d[0]), 0) < d[1]:
+                eng[q].wait_ge(T.sem[d[0]], d[1])
+                seen[(q, d[0])] = d[1]
 
-    def mark(q, ins):
-        ins.then_inc(T.sem[q + "s"], 1)
-        done[q] += 1
-        return (q, done[q])
+    banks = 7 if rank else 8
+    users, turn, bank, own = [[] for _ in range(8)], [0], {}, {}
+    B = range(4)
 
-    far = cores[mirror[0]] if topo.chip(core) == topo.chip(cores[0]) else cores[0]
-    near = [c for c in topo.cores_of(core) if c != core][0]
-    ALL = topo.engines(core, near)
-    OFF = topo.engines(core, far)
-    ON = [e for e in ALL if e not in OFF]
-    nALL, nOFF, nON = len(ALL), len(OFF), len(ON)
+    def view(name, a, n):
+        v = T[name][:, a:a + n]
+        return v.bitcast(dt.uint8) if SCRATCH[name][2] == F8 else v
 
-    def ids(dsts):
+    def step(q, s):
+        n = s[0]
+        if q == "g":
+            piece, ways = s
+            sem, parts = pieces(piece, me, role[core])
+
+            def call():
+                for k, (a, b, ca, _, w) in enumerate(parts):
+                    g.remote_dma_fused([RemoteDMATransfer(
+                        dst_ids=[DstId(rid=topo.addr(d)[0], pnc=topo.addr(d)[1]) for d in ds], dma_engine_mask=sum(1 << e for e in es),
+                        remote_sem=T.sem[sem], srcs=[view(a, ca, w)], dsts=[view(b, pieces(piece, me, role[d])[1][k][3], w) for d in ds])
+                        for es, ds in ways], local_sem=T.sem.sent)
+                    sent[0] += sum(len(es) for es, _ in ways)
+            if piece[0][:2] in ("kc", "ks", "kk"):
+                return [d for a, _, ca, _, w in parts for b in range(ca // 128, (ca + w) // 128) for d in block[a, b]], call, []
+            if piece[0] == "kp" and rank:
+                return ["l_p"], call, []
+            return [("Z", u) for u in range(piece[2], piece[3])] if piece[0] == "a" else [sem], call, []
+        if n == "Q":
+            if s[1] == "k":
+                a, e = 128 * int(s[2]), 128 * int(s[3])
+                return ["l_" + s[1:3]], lambda: g.vector.quantize_mx(T.kc[:, a:e], T.ks[:, a:e], T.kt[:, 4 * a:4 * e]), [s[1:]]
+            name, c, p, a, src = {"r": ("r", "rc", "rp", 0, T.rtt[:]), "x": ("x%d" % me, "xc", "xp", 2 * TQ, T.xt[:]),
+                                  "v": ("v%d" % keys, "vc", "vp", 128 * keys, T.vt[:])}[s[1:]]
+            w = src.shape[1] // 4
+            return ["l_" + s[1:]], lambda: g.vector.quantize_mx(T[c][:, a:a + w], T[p][:, a:a + w], src), [name]
+        if n == "C":
+            a = 32 * int(s[1])
+            return ["l_q"], lambda: g.vector.tensor_copy(T.qpi[a:a + 32, 32:48], T.qpi[0:32, 32:48]), ["q%d" % me]
+        if n == "F":
+            a = int(s[1])
+            return (["l_p" if rank and not a else "kp"], lambda: g.vector.tensor_scalar(T.kf[:, a:a + 4], T.kpi[:, a:a + 4], 128.0, None, SUB),
+                    [("kf", a // 4)])
+        if n == "l":
+            (u0, u1), b = SPAN[s[1]], int(s[2])
+            us = range(u0, u1)
+            return ([("kf", b // 4)] + ["q%d" % place[u // 2] for u in us],
+                    lambda: g.vector.tensor_scalar(T.of[:, 48 * b + 8 * u0:48 * b + 8 * u1], T.qpi[:, 8 * u0:8 * u1], T.kf[:, b:b + 1], 255.0, SUB, MIN),
+                    [("of", b, u) for u in us])
+        if n in "PS":
+            b = int(s[-1])
+            k = turn[0] % banks
+            deps = block["kc", b] + block["ks", b] + users[k]
+            if n == "P":
+                deps, c, p, a, w, drains = deps + ["r"], "rc", "rp", 0, TQ, [("W", b)]
+            else:
+                us = range(*SPAN[s[1]])
+                deps, c, p, a, w = deps + ["x%d" % place[u // 2] for u in us], "xc", "xp", U * us[0], U * len(us)
+                drains = [("A", b, u) for u in us]
+
+            def call():
+                turn[0] += 1
+                users[k] = drains
+                for d in drains:
+                    bank[d] = (k, a)
+                return g.tensor.matmul_mx(T["ps%d" % k][:, 0:w], T.kc[:, 128 * b:128 * b + 128], T.ks[:, 128 * b:128 * b + 128],
+                                          T[c][:, a:a + w], T[p][:, a:a + w], True, True)
+            return deps, call, [("mm",) + d for d in drains]
+        if n == "W":
+            b = int(s[1])
+
+            def call():
+                d, p = T.pw[:, TQ * b:TQ * b + TQ], T["ps%d" % bank["W", b][0]][:, 0:TQ]
+                return g.vector.tensor_copy(d, p) if q == "v" else g.scalar.activation(d, p, COPY)
+            return [("mm", "W", b)], call, [("W", b)]
+        if n == "Y":
+            r, start, stop = s[1:]
+            return (["v%d" % r] + [d for d in ("a%d" % r,) if d in due] + own.get(r, []),
+                    lambda: g.tensor.matmul_mx(T.ps7[:, 0:TQ], T.vc[:, 128 * r:128 * r + 128], T.vp[:, 128 * r:128 * r + 128],
+                                               T.ac[:, TQ * r:TQ * r + TQ], T.ap[:, TQ * r:TQ * r + TQ], start, stop), ["y"] if stop else [])
+        if n == "O":
+            return ["y"], lambda: g.scalar.activation(T.ys[:], T.ps7[:, 0:TQ], COPY), ["out"]
+        u0, u1 = SPAN[s[1]]
+        us = range(u0, u1)
+        b = int(s[2])
+        h0 = 12 * TQ * (b // 4)
+        if n == "Z":
+            r = far[me] if b else keys
+            c, p, a = ("ac", "ap", TQ * r + U * (u0 % 2)) if rank and u0 >= 4 else ("oc", "op", U * u0)
+            w = U * (u1 - u0)
+            return ([("R", e, u) for e in range(b, b + 4) for u in us],
+                    lambda: g.vector.quantize_mx(T[c][:, a:a + w], T[p][:, a:a + w], T.ht[:, h0 + 4 * U * u0:h0 + 4 * U * u1]),
+                    [("Z", u + 6 * (b // 4)) for u in us])
+        if n == "G":
+
+            def call():
+                o, w = T.gg[:, 768 * b + U * u0:768 * b + U * u1], T.pw[:, TQ * b:TQ * b + TQ].indirect(T.of[:, 48 * b + 8 * u0:48 * b + 8 * u1])
+                return g.vector.tensor_copy(o, w) if q == "v" else g.scalar.activation(o, w, COPY)
+            return [("W", b)] + [("of", b, u) for u in us], call, [("G", b, u) for u in us]
+        if n == "A":
+
+            def call():
+                k, a = bank["A", b, u0]
+                return g.vector.tensor_tensor(T.ht[:, h0 + 4 * U * u0 + b % 4:h0 + 4 * U * u1:4], T["ps%d" % k][:, U * u0 - a:U * u1 - a],
+                                              T.gg[:, 768 * b + U * u0:768 * b + U * u1], ADD)
+            return [("mm", "A", b, u) for u in us] + [("G", b, u) for u in us], call, [("A", b, u) for u in us]
+        st = int(s[3])
+        h = T.ht[:, h0 + 4 * U * u0 + b % 4:h0 + 4 * U * u1:st]
+        part = [(c, u) for c in range(b, b // 4 * 4 + 4, st) for u in us]
+        return ([("A",) + k for k in part],
+                lambda: g.vector.tensor_scalar(h, h, 0.0, 0.03125, MAX, MULT) if q == "v" else g.scalar.activation(h, h, RELU, scale=0.03125),
+                [("R",) + k for k in part])
+
+    def run(queues):
+        while any(queues.values()):
+            moved = False
+            for q, l in queues.items():
+                while l:
+                    deps, call, gives = step(q, l[0])
+                    if not all(d in at for d in deps):
+                        break
+                    after(q, [at[d] for d in deps])
+                    ins = call()
+                    if q != "g":
+                        ins.then_inc(T.sem[q + "s"], 1)
+                        count[q] += 1
+                        for k in gives:
+                            at[k] = (q + "s", count[q])
+                    l.pop(0)
+                    moved = True
+            assert moved, (core, queues)
+
+    def cfg(q):
         out = []
-        for d in dsts:
-            rid, pid = topo.addr(d)[:2]
-            out.append(DstId(rid=rid, pnc=pid))
+        for s in CFG.get("%s%d.%s" % (kind, idx, q), CFG.get(kind + "." + q)).split():
+            out += ["l%s%d" % (s[1], int(s[2]) + b) for b in B] if s[0] == "L" else [s]
         return out
 
-    def send(sems, src, *ways):
-        if not isinstance(sems, list):
-            sems = [sems] * len(ways)
-        g.remote_dma_fused([RemoteDMATransfer(dst_ids=ids(ds), dma_engine_mask=sum(1 << e for e in es), remote_sem=T.sem[sem],
-                                              srcs=[src], dsts=[to] * len(ds)) for sem, (es, ds, to) in zip(sems, ways)], local_sem=T.sem.sent)
-        sent[0] += sum(len(es) for es, _, _ in ways)
-
-    def codes(name, a, b):
-        return T[name][:, a:b].bitcast(dt.uint8)
-
-    def plane(name, a, b):
-        return T[name][:, a:b]
-
-    def ship(sems, src, a, n, *ways):
-        for k, view in ((0, codes), (1, plane)):
-            send(sems, view(src[k], a, a + n), *[(es, ds, view(to[k], ta, ta + n)) for es, ds, to, ta in ways])
-
-    M, KO, KF = ("mc", "mp"), ("kco", "kpo"), ("kcf", "kpf")
-
-    def V(s):
-        return ("vc%d" % s, "vp%d" % s)
-
-    def A(s):
-        return ("ac%d" % s, "ap%d" % s)
-
-    def quantise(to, a, b, src, *deps):
-        after("v", *deps)
-        return mark("v", g.vector.quantize_mx(T[to[0]][:, a:b], T[to[1]][:, a:b], src))
-
-    def lists(n, kf, a, w, *deps):
-        after("v", *deps)
-        for b in range(4):
-            m = mark("v", g.vector.tensor_scalar(T["ot" + n][:, w * b:w * b + w], T.qpi[:, a:a + w], T[kf][:, b:b + 1], 0.0, SUB, MAX))
-        after("v", m)
-        return mark("v", g.vector.tensor_scalar(T["of" + n][:], T["ot" + n][:], 255.0, None, MIN))
-
-    banks = 7 if rank is not None else 8
-    drained, turn = [()] * 8, [0]
-    P, W, S, G, R = {}, {}, {}, {}, {}
-
-    def product(K, b, a):
-        k = turn[0] % banks
-        turn[0] += 1
-        after("t", *drained[k])
-        return k, mark("t", g.tensor.matmul_mx(T["ps%d" % k][:, 0:TQ], T[K[0]][:, 128 * b:128 * b + 128], T[K[1]][:, 128 * b:128 * b + 128],
-                                               T.mc[:, a:a + TQ], T.mp[:, a:a + TQ], True, True))
-
-    def distances(n, K, bs, *deps):
-        after("t", *deps)
-        for b in bs:
-            P[n, b] = product(K, b, RT)
-
-    def scores(i, K, a, *deps):
-        after("t", *deps)
-        for b in range(4):
-            S[i, b] = product(K, b, a)
-
-    def window(n, b, q):
-        k, m = P[n, b]
-        d, p = T["pw" + n][:, TQ * b:TQ * b + TQ], T["ps%d" % k][:, 0:TQ]
-        after(q, m)
-        W[n, b] = mark(q, g.vector.tensor_copy(d, p) if q == "v" else g.scalar.activation(d, p, COPY))
-        drained[k] = (W[n, b],)
-
-    def pick(i, n, b, of, col, li):
-        after("s", W[n, b], li)
-        G[i, b] = mark("s", g.scalar.activation(T["gg%d" % i][:, TQ * b:TQ * b + TQ],
-                                                T["pw" + n][:, TQ * b:TQ * b + TQ].indirect(T[of][:, col:col + 16]), COPY))
-
-    def add(i, b):
-        k, m = S[i, b]
-        after("v", m, G[i, b])
-        R[i, b] = mark("v", g.vector.tensor_tensor(T["ht%d" % i][:, b:4 * TQ:4], T["ps%d" % k][:, 0:TQ], T["gg%d" % i][:, TQ * b:TQ * b + TQ], ADD))
-        drained[k] = (R[i, b],)
-
-    def relu(i, b, step):
-        after("v", *[R[i, c] for c in range(b, 4, step)])
-        h = T["ht%d" % i][:, b:4 * TQ:step]
-        R[i] = mark("v", g.vector.tensor_scalar(h, h, 0.0, 0.03125, MAX, MULT))
-
-    def pack(i, to):
-        return quantise(to, 0, TQ, T["ht%d" % i][:], R[i])
-
-    def lace(i, j, to):
-        add(j, 0)
-        relu(i, 0, 1)
-        add(j, 1)
-        m = pack(i, to)
-        add(j, 2)
-        return m
-
-    def close(i, to):
-        relu(i, 0, 2)
-        add(i, 3)
-        relu(i, 1, 2)
-        return pack(i, to)
-
-    def farewell():
-        after("g", ("v", done["v"]), ("s", done["s"]), ("t", done["t"]), ("sent", sent[0]))
-
-    B = range(4)
-    QIN = ("q_in", nON + nOFF)
-    if rank is None:
-        here, home = [cores[r]], [cores[q] for q in local[r]]
-        KFIN = ("kf_in", nOFF)
-        after("g", KFIN)
-        send("kf_in", T.kff[:], (ALL, here, T.kff[:]))
-        for i in range(2):
-            after("g", ("k%d_in" % i, 2 * nOFF))
-            ship("k%d_in" % i, KF, 256 * i, 256, (ALL, here, KF, 256 * i))
-        after("g", ("v_in%d" % far_s, 2 * nOFF))
-        ship("v_in%d" % far_s, V(far_s), 0, 128, (ALL, home, V(far_s), 0))
-
-        li = lists("x", "kff", 16, 32, QIN, KFIN)
-        distances("f", KF, (0, 1), ("r_in", 2 * nON), ("k0_in", 2 * nOFF))
-        distances("f", KF, (2, 3), ("k1_in", 2 * nOFF))
-        window("f", 0, "s")
-        for b in (1, 2, 3):
-            window("f", b, "v")
-        for i in range(2):
-            for b in B:
-                pick(i, "f", b, "ofx", 32 * b + 16 * i, li)
-        scores(0, KF, PRV, ("xp_in", 2 * nON))
-        for b in B:
-            add(0, b)
-        scores(1, KF, NXT, ("xn_in", 2 * nOFF))
-        made = [lace(0, 1, ("oc0", "op0")), close(1, ("oc1", "op1"))]
-        for i, q in ((0, prv), (1, nxt)):
-            after("g", made[i])
-            ship("a_in%d" % far_s, ("oc%d" % i, "op%d" % i), 0, TQ, (ALL, [cores[q]], A(far_s), 0))
-        farewell()
-        return
-
-    away, mine = [worker[far_s]], [worker[r]]
-    to_nxt, to_prv = [cores[nxt], worker[nxt]], [cores[prv], worker[prv]]
-    g.sync.dma_start(T.kpi[:], T.kp[:]).then_inc(T.sem.l_p, 16)
-    for i in range(2):
-        g.sync.dma_start(T.kt[:, 1024 * i:1024 * i + 1024], T.ky[:, 1024 * i:1024 * i + 1024]).then_inc(T.sem["l_k%d" % i], 16)
-    g.sync.dma_start(T.rtt[:], T.rt[:]).then_inc(T.sem.l_r, 16)
-    for k in range(8):
-        g.scalar.dma_start(T.qpi[16 * k:16 * k + 16, 0:16], T.qp[:]).then_inc(T.sem.l_q, 16)
-    g.scalar.dma_start(T.xt[:], T.qx[:]).then_inc(T.sem.l_x, 16)
-    g.scalar.dma_start(T.vt[:], T.vv[:]).then_inc(T.sem.l_v, 16)
-    LQ = ("l_q", 16 * 8)
-
-    after("v", ("l_p", 16))
-    mf = mark("v", g.vector.tensor_scalar(T.kfo[:], T.kpi[:], 128.0, None, SUB))
-    after("g", mf)
-    send("kf_in", T.kfo[:], (OFF, away, T.kff[:]))
-    after("g", LQ)
-    send("q_in", T.qpi[:, 0:16], (ON, to_nxt, T.qpi[:, 16:32]), (OFF, to_prv, T.qpi[:, 32:48]))
-    for i in range(2):
-        mk = quantise(KO, 256 * i, 256 * i + 256, T.kt[:, 1024 * i:1024 * i + 1024], ("l_k%d" % i, 16))
-        after("g", mk)
-        ship("k%d_in" % i, KO, 256 * i, 256, (OFF, away, KF, 256 * i))
-    lo = lists("o", "kfo", 0, 16, mf, LQ)
-    mr = quantise(M, RT, RT + TQ, T.rtt[:], ("l_r", 16))
-    after("g", mr)
-    ship("r_in", M, RT, TQ, (ON, mine, M, RT))
-    mx = quantise(M, OWN, OWN + TQ, T.xt[:], ("l_x", 16))
-    after("g", mx)
-    ship(["xp_in", "xn_in"], M, OWN, TQ, (ON, to_nxt, M, PRV), (OFF, to_prv, M, NXT))
-
-    distances("o", KO, B, mk, mr)
-    for b, q in ((0, "s"), (1, "s"), (2, "v"), (3, "v")):
-        window("o", b, q)
-    scores(0, KO, OWN, mx)
-    for b in B:
-        pick(0, "o", b, "ofo", 16 * b, lo)
-    add(0, 0)
-    lx = lists("x", "kfo", 16, 32, QIN)
-    for i in range(2):
-        for b in B:
-            pick(1 + i, "o", b, "ofx", 32 * b + 16 * i, lx)
-    add(0, 1)
-    mv = quantise(V(r), 0, 128, T.vt[:], ("l_v", 16))
-    after("g", mv)
-    ship("v_in%d" % r, V(r), 0, 128, (OFF, away, V(r), 0), (ON, [cores[nxt], cores[prv]], V(r), 0))
-    add(0, 2)
-    add(0, 3)
-    scores(1, KO, PRV, ("xp_in", 2 * nON))
-    made = {r: lace(0, 1, A(r))}
-    lf = lists("f", "kff", 0, 16, ("kf_in", nALL))
-    add(1, 3)
-    scores(2, KO, NXT, ("xn_in", 2 * nOFF))
-    m1 = lace(1, 2, ("oc0", "op0"))
-    add(2, 3)
-    relu(2, 0, 1)
-    m2 = pack(2, ("oc1", "op1"))
-    for i, q, m in ((0, prv, m1), (1, nxt, m2)):
-        after("g", m)
-        ship("a_in%d" % r, ("oc%d" % i, "op%d" % i), 0, TQ, (ALL, [cores[q]], A(r), 0))
-
-    order = [r, nxt, prv, mirror[nxt], far_s, mirror[prv]]
-
-    def value(s):
-        after("t", mv if s == r else ("v_in%d" % s, 2 * (nON if s in (prv, nxt) else nALL)))
-        after("t", made[s] if s in made else ("a_in%d" % s, 2 * nALL))
-        return mark("t", g.tensor.matmul_mx(T.ps7[:, 0:TQ], T["vc%d" % s][:], T["vp%d" % s][:], T["ac%d" % s][:], T["ap%d" % s][:],
-                                            s == order[0], s == order[-1]))
-
-    value(r)
-    distances("f", KF, (0, 1), ("k0_in", 2 * nALL))
-    distances("f", KF, (2, 3), ("k1_in", 2 * nALL))
-    for b, q in ((0, "s"), (1, "s"), (2, "v"), (3, "v")):
-        window("f", b, q)
-    for b in B:
-        pick(3, "f", b, "off", 16 * b, lf)
-    scores(3, KF, OWN)
-    for b in range(3):
-        add(3, b)
-    made[far_s] = close(3, A(far_s))
-    for s in order[1:]:
-        m = value(s)
-    after("s", m)
-    m = mark("s", g.scalar.activation(T.ys[:], T.ps7[:, 0:TQ], COPY))
-    after("s", m)
-    g.scalar.dma_start(T.y[:], T.ys[:]).then_inc(T.sem.stored, 16)
-    after("g", ("stored", 16))
-    farewell()
+    queues = {q: cfg(q) for q in "vst"}
+    queues["g"] = list(calls[core])
+    if rank:
+        for s in queues["v"]:
+            if s[0] == "Z" and SPAN[s[1]][0] >= 4:
+                own.setdefault(far[me] if int(s[2]) else keys, []).extend(("Z", u + 6 * (int(s[2]) // 4)) for u in range(*SPAN[s[1]]))
+            if s[:2] == "Qk":
+                for b in range(int(s[2]), int(s[3])):
+                    block["kc", b] = block["ks", b] = [s[1:]]
+        g.sync.dma_start(T.kpi[:, 0:4], T.kp[:]).then_inc(T.sem.l_p, 16)
+        for k in range(2):
+            g.scalar.dma_start(T.qpi[16 * k:16 * k + 16, 32:48], T.qp[:]).then_inc(T.sem.l_q, 16)
+        src = {"r": (T.rtt[:], T.rt[:]), "x": (T.xt[:], T.qx[:]), "v": (T.vt[:], T.vv[:])}
+        for n in CFG.get("loads%d" % me, CFG["loads"]).split():
+            if n[0] == "k":
+                a, e = 512 * int(n[1]), 512 * int(n[2])
+                src[n] = (T.kt[:, a:e], T.ky[:, a:e])
+            g.sync.dma_start(*src[n]).then_inc(T.sem["l_" + n[:2]], 16)
+            at["l_" + n[:2]] = ("l_" + n[:2], 16)
+        at["l_q"], at["l_p"] = ("l_q", 32), ("l_p", 16)
+        order = [(home if s[0] == "C" else far)[place["pni".index(s[1])]] for s in cfg("y")]
+        ys = [("Y", r, r == order[0], r == order[-1]) for r in order]
+        queues["t"] = [ys.pop(0) if s == "Y" else s for s in queues["t"]] + ys
+        run(queues)
+        after("s", [at["out"]])
+        g.scalar.dma_start(T.y[:], T.ys[:]).then_inc(T.sem.stored, 16)
+        after("g", [("stored", 16)])
+    else:
+        run(queues)
+    after("g", [(q + "s", count[q]) for q in count] + [("sent", sent[0])] + [(s, due[s]) for s in due])

@@ -8,11 +8,11 @@ SCRATCH = {
     "xt": ("sbuf", [128, 1024], "bfloat16"),
     "rtt": ("sbuf", [128, 1024], "bfloat16"),
     "vt": ("sbuf", [128, 512], "bfloat16"),
-    "rc": ("sbuf", [128, TQ], F8), "rp": ("sbuf", [128, TQ], "uint8"),
-    "xc": ("sbuf", [128, 3 * TQ], F8), "xp": ("sbuf", [128, 3 * TQ], "uint8"),
-    "kc": ("sbuf", [128, 1024], F8), "ks": ("sbuf", [128, 1024], "uint8"),
+    "mc": ("sbuf", [128, 4 * TQ], F8), "mp": ("sbuf", [128, 4 * TQ], "uint8"),
+    "kc": ("sbuf", [128, 1280], F8), "ks": ("sbuf", [128, 1280], "uint8"),
     "kpi": ("sbuf", [128, 8], "int32"), "kf": ("sbuf", [128, 8], "float32"),
-    "qpi": ("sbuf", [128, 48], "int32"),
+    "qld": ("sbuf", [128, 16], "int32"), "qpi": ("sbuf", [128, 48], "uint16"),
+    "og": ("sbuf", [128, 128], "uint16"),
     "of": ("sbuf", [128, 8 * 48], "uint16"),
     "pw": ("sbuf", [128, 8 * TQ], "float32"),
     "gg": ("sbuf", [128, 24 * TQ], "float32"),
@@ -25,7 +25,7 @@ SCRATCH = {
 for _i in range(8):
     SCRATCH["ps%d" % _i] = ("psum", [128, 512], "float32")
 
-SEMAPHORES = (["l_p", "l_q", "l_v", "l_r", "l_x", "vs", "ss", "ts", "sent", "stored", "kp", "r"]
+SEMAPHORES = (["l_p", "l_q", "l_v", "l_r", "l_x", "vs", "ss", "ts", "sent", "stored", "kp", "r", "og", "t1", "t2", "kfs", "kgs", "rx"]
               + ["%s%d" % (n, i) for n in ("kc", "ks", "kk", "l_k") for i in range(4)]
               + ["%s%d" % (n, i) for n in "qx" for i in range(3)] + ["%s%d" % (n, i) for n in "va" for i in range(NR)])
 SPAN = {"p": (0, 2), "n": (2, 4), "i": (4, 6), "w": (0, 4), "z": (2, 6), "a": (0, 6),
@@ -42,6 +42,85 @@ CFG = {
     "first.s": "W0 Gp0 Gp1 Gn0 Gn1 W2 Gp2 Gp3 Gn2 Gn3",
     "first.t": "P0 P1 Sp0 Sp1 Sn0 Sn1 P2 P3 Sp2 Sp3 Sn2 Sn3",
 }
+CFG["rank.v"] = "C0 " + CFG["rank.v"]
+CFG.update({
+    "rank.g": "kp OFF A; q ON Fn Cn Cp Fp; kk02 OFF A; x ON Fn; r ON Fi; x ON Cn; ks24 OFF A; kc23 OFF A; kc34 OFF A; x ON Fp / OFF Cp; v OFF A / ON Cn Cp; ap ALL Cp; an ALL Cn",
+    "first.t": "P0 P1 Sp0 Sp1 Sn0 Sn1 P2 Sp2 Sn2 P3 Sp3 Sn3",
+    "first.s": "W0 Gp0 Gp1 Gn0 Gn1 W2 Gp2 Gn2 W3 Gp3 Gn3",
+    "first.v": "F0 Lw0 W1 Ap0 Ap1 An0 Rw04 An1 Rw14 Ap2 An2 Rw24 Ap3 Rp34 Zp0 An3 Rn34 Zn0",
+})
+CFG.update({
+    "loads": "k02 r x k24 v",
+    "rank.g": "kp OFF A; q ON Fn Cn Cp Fp; kc01 OFF A; r ON Fi; x ON Fn; ks04 OFF A; kc12 OFF A; x ON Cn; kc23 OFF A; kc34 OFF A; x ON Cp; v OFF A / ON Cn Cp; ap ALL Cp; an ALL Cn",
+    "first.g": "kf ALL Ci; xp ALL Fn; kc02 ALL Ci; ks04 ALL Ci; kc23 ALL Ci; kc34 ALL Ci; v ALL C0 C1 C2; ap ALL Cp; an ALL Cn",
+    "first.v": "F0 Lw0 Gn0 Ap0 Rp04 Gn1 Ap1 Rp14 An1 An0 An2 Ap2 Rn14 Rp24 Ap3 Rn24 An3 Rn04 Zp0 Zn0",
+    "first.s": "W0 Gp0 W1 Gp1 W2 Gn2 Gp2 W3 Gp3 Gn3 Rp34 Rn34",
+    "first.t": "P0 Sp0 P1 Sp1 P2 Sn0 Sn1 Sn2 Sn3 P3 Sp2 Sp3",
+    "rank.v": "C0 C1 C2 C3 F0 Qk02 Li0 Qr Qx Qk24 Qv Gi0 Ai0 Lw0 Gp0 Ai1 Ai2 Gn3 Gp2 Ai3 Gn0 Li4 Ap3 Ap1 Ap0 Ap2 An0 Rp02 An2 An3 An1 Rn02 Rn12 Zp0 Zn0 Zi0 Ai4 Ai6 Ai7 Ai5 Ri54 Zi4",
+    "rank.s": "W0 W1 W2 Gi1 W3 Gi2 Gn2 Gi3 Gp1 Ri02 Gp3 Gn1 Ri12 Rp12 W4 W5 W6 Gi4 Gi5 W7 Gi6 Gi7 Ri44 Ri64 Ri74 O01",
+    "rank.t": "P0 P1 Si0 P2 Si1 P3 Si2 Si3 Sp3 Sp1 Sp0 Sp2 Sn3 Sn0 P4 Sn2 P5 P6 Sn1 P7 Si4 Si6 Si5 Si7",
+    "rank.y": "Ci Cn Fn Cp Fi Fp",
+})
+CFG.update({
+    "first0.g": "kf ALL Ci; xp ALL Fn; kc02 ALL Ci; ks04 ALL Ci; kc24 ALL Ci; v ALL C0 C1 C2; ap ALL Cp; an ALL Cn",
+    "first.g": "kf ALL Ci; xp ALL Fn; ks04 ALL Ci; kc13 ALL Ci; kc01 ALL Ci; kc34 ALL Ci; v ALL C0 C1 C2; ap ALL Cp; an ALL Cn",
+    "rank0.g": "kp OFF A; q ON Fn Cn Cp Fp; kc02 OFF A; rx ON Fn; ks04 OFF A; x ON Cn; kc24 OFF A; x ON Cp; tb1 OFF A1; tb2 OFF A2; v OFF A / ON Cn Cp; ap ALL Cp; an ALL Cn",
+    "rank1.g": "kp OFF A; q ON Fn Cn Cp Fp; kc12 LO A; ta1 HI C0; rx ON Fn; ks04 OFF A; x ON Cn; kc23 OFF A; kc34 OFF A; x ON Cp; v OFF A / ON Cn Cp; ap ALL Cp; an ALL Cn",
+    "rank2.g": "kp OFF A; q ON Fn Cn Cp Fp; kc12 LO A; ta2 HI C0; rx ON Fn; ks04 OFF A; x ON Cn; kc23 OFF A; kc34 OFF A; x ON Cp; v OFF A / ON Cn Cp; ap ALL Cp; an ALL Cn",
+    "first.v": "F0 Lw0 W1 Gp1 Ap1 Rp14 Gn2 Ap2 Gp0 An2 Ap0 An1 An0 Ap3 Rp04 Rn14 An3 Zp0 Rn24 Zn0",
+    "first.s": "Gn1 W2 Gp2 W0 W3 Gn0 Gp3 Rp24 Gn3 Rp34 Rn04 Rn34",
+    "first.t": "P1 Sp1 P2 Sp2 P0 P3 Sn1 Sn2 Sp0 Sp3 Sn3 Sn0",
+    "first0.v": "F0 Lw0 W1 W2 W3 Gw1 Ap0 Ap1 Ap2 Ap3 An0 An2 An1 An3 Zp0 Rn12 Zn0",
+    "first0.s": "W0 Gw0 Gw2 Gw3 Rp01 Rn02",
+    "first0.t": "P0 P1 P2 P3 Sp2 Sp3 Sp1 Sp0 Sn2 Sn0 Sn3 Sn1",
+    "rank.v": "C0 C1 C2 C3 F0 Qk02 Li0 Qr Qx Qk24 Qv Gi1 Ai1 Gi2 Lw0 Ai2 Ai0 Ai3 Gw2 Li4 Ap0 Ap1 Ap2 Ap3 An1 An2 An0 An3 Zp0 Rn01 Zi0 Zn0 Gi7 Ai6 Ai7 Ai5 Ai4 Ri42 Zi4",
+    "rank.s": "W1 W0 W2 W3 Gi0 Gi3 Gw1 Gw0 Gw3 Ri01 Rp01 W5 W6 W7 Gi6 W4 Gi5 Gi4 Ri52 O01",
+    "rank.t": "P1 P0 P2 Si1 P3 Si0 Si3 Si2 Sp0 Sp1 Sp2 Sp3 Sn1 Sn2 Sn0 P5 Sn3 P6 P7 Si5 Si6 Si7 Si4 P4",
+    "rank.y": "Ci Cn Cp Fn Fi Fp",
+})
+for _k in list(CFG):
+    if _k.endswith(".g"):
+        CFG[_k] = CFG[_k].replace("q ON Fn Cn Cp Fp", "q ON Fn Cn Cp Fi").replace("kf ALL Ci; xp ALL Fn", "qp ALL Fn; xp ALL Fn; og ALL Ci")
+CFG.update({
+    "first.v": "F0 Lp0 H Ln0 Gn1 Ap1 Rp14 Gp2 An1 Ap2 An2 Gp3 Ap0 Ap3 Rp04 Rp24 An3 An0 Zp0 Rn04 Zn0",
+    "first.s": "W1 Gp1 W2 Gn2 W0 W3 Gp0 Gn0 Gn3 Rp34 Rn24 Rn34 Rn14",
+    "first.t": "P1 Sp1 P2 Sp2 P0 Sn1 P3 Sn2 Sp0 Sn3 Sp3 Sn0",
+    "first0.v": "F0 Lp0 H Ln0 W1 W2 W3 Gw1 Ap0 Ap1 Ap2 Ap3 An0 An2 An1 An3 Zp0 Rn12 Zn0",
+    "rank.v": "C0 C1 C2 C3 Qk02 Qr F0 Qx li1 Qk24 Qv li0 li2 li3 W2 Ai1 Lw0 Gi3 Ai0 Gw2 Ai3 Ai2 Ap0 Ap2 Ap1 Ap3 An3 An0 An2 An1 Zi0 Zp0 Rn01 Zn0 Gi7 Ai5 Ai7 Ai4 Ai6 Ri42 Zi4",
+    "rank.s": "W1 W0 Gi1 W3 Gi0 Gi2 Gw0 Gw3 Gw1 Ri01 Rp01 W5 W4 W7 Gi5 W6 Gi4 Gi6 Ri52 O01",
+    "rank.t": "P1 P0 P2 P3 Si1 Si2 Si0 Si3 Sp0 Sp2 Sp1 Sp3 Sn3 Sn2 Sn0 Sn1 P4 P5 Si6 Si7 P7 Si5 P6 Si4",
+})
+for _k in list(CFG):
+    if _k.endswith(".g"):
+        CFG[_k] = (CFG[_k].replace("q ON Fn Cn Cp Fi", "q ON Fn Cn Cp").replace("qp ALL Fn;", "qp ALL Fn Fp;")
+                   .replace("og ALL Ci; ks04 ALL Ci; kc13 ALL Ci;", "ks04 ALL Ci; kc13 ALL Ci; og ALL Ci;")
+                   .replace("og ALL Ci; kc02 ALL Ci; ks04 ALL Ci; kc24 ALL Ci", "kc02 ALL Ci; ks04 ALL Ci; kc24 ALL Ci; og ALL Ci"))
+    if _k.endswith(".v"):
+        CFG[_k] = CFG[_k].replace("Lp0 H Ln0", "Lp0 Ln0 H")
+CFG.update({
+    "rank.v": "C0 C1 C2 C3 F0 Qk02 Li0 Qr Qx Qk24 Qv Gi0 Lw0 Gw0 Ai2 Ai0 Gw2 Ai1 Ai3 Ap3 Ap0 Ap2 Ap1 An0 An3 An1 An2 Zp0 Rn01 Zi0 Zn0 Gi7 Ai5 Ai7 Ai4 Ai6 Ri42 Zi4",
+    "rank.s": "W0 W1 W2 W3 Gi2 Gi1 Gw3 Gi3 Gw1 Ri01 Rp01 W6 W5 W7 W4 Gi5 Gi4 Gi6 Ri52 O01",
+    "rank.t": "P0 P1 P2 P3 Si0 Si2 Si1 Si3 Sp3 Sp0 Sp2 Sp1 Sn0 Sn2 Sn3 Sn1 P6 P5 Si5 P7 Si6 P4 Si7 Si4",
+})
+CFG.update({
+    "rank.v": "C0 C1 C2 C3 F0 Qk02 Li0 Qr Qx Qk24 Qv Gi0 Ai0 Lw0 Gw0 Ai1 Ai2 Gw2 Ai3 Ap0 Ap2 Ap3 Ap1 An0 Rp01 An2 Zp0 An3 An1 Rn01 Zn0 Zi0 Ai5 Ai6 Ai4 Ai7 Ri52 Zi4",
+    "rank.s": "W0 W1 W2 W3 Gi1 Gi2 Gi3 Gw3 Gw1 Ri01 W5 W6 Gi5 Gi6 W4 Gi4 W7 Gi7 Ri42 O01",
+    "rank.t": "P0 P1 Si0 P2 P3 Si1 Si2 Si3 Sp0 Sp2 Sp3 Sp1 Sn0 Sn2 P5 P6 Sn3 Sn1 P4 P7 Si5 Si6 Si4 Si7",
+})
+CFG.update({
+    "first0.g": "qp ALL Fn X2; kg ALL X1; xp ALL Fn; kc02 ALL Ci; ks04 ALL Ci; kc24 ALL Ci; v ALL C0 C1 C2; ap ALL Cp; an ALL Cn",
+    "first1.g": "qp ALL Fn X1; kf ALL X1; xp ALL Fn; ks04 ALL Ci; kc13 ALL Ci; kc01 ALL Ci; kc34 ALL Ci; v ALL C0 C1 C2; ap ALL Cp; an ALL Cn",
+    "first2.g": "qp ALL Fn X1; kf ALL X2; xp ALL Fn; ks04 ALL Ci; kc13 ALL Ci; kc01 ALL Ci; kc34 ALL Ci; v ALL C0 C1 C2; ap ALL Cp; an ALL Cn",
+    "second1.g": "og ON C1; oh ON C0", "second2.g": "og ON C2",
+    "second1.v": "H J", "second2.v": "H", "second.s": "", "second.t": "",
+    "first.v": "F0 Lp0 Ln0 Gn1 Ap1 Rp14 Gp2 An1 Ap2 An2 Gp3 Ap0 Ap3 Rp04 Rp24 An3 An0 Zp0 Rn04 Zn0",
+    "first0.v": "F0 Lp0 Ln0 W1 W2 W3 Gw1 Ap0 Ap1 Ap2 Ap3 An0 An2 An1 An3 Zp0 Rn12 Zn0",
+})
+CFG.update({
+    "first0.v": "F0 Lp0 Ln0 Gn1 Gp0 Gp3 Ap0 Ap1 Ap3 An1 Ap2 An3 Rp12 An0 An2 Zp0 Rn02 Zn0",
+    "first0.s": "W1 W0 W3 W2 Gp1 Gp2 Gn3 Gn0 Gn2 Rp02 Rn12",
+    "first0.t": "P1 P0 P3 P2 Sp0 Sp1 Sp3 Sn1 Sp2 Sn3 Sn0 Sn2",
+})
 
 
 def layout(T, topo):
@@ -88,8 +167,9 @@ def plan(T, topo):
                     keys, me = (home if w[0] == "C" else far)[at[w[1]]], at[w[1]]
                 role[c] = (kind, keys, me, home, far, i)
                 calls[c] = []
-                for text in text.split(";"):
-                    name, rest = text.split(None, 1)
+                for text in filter(None, text.replace("&", ";&").split(";")):
+                    name, rest = text.strip("&").split(None, 1)
+                    name, _, part = name.partition(".")
                     ways = [(E[w.split()[0]], [who[d] for d in w.split()[1:]]) for w in rest.split("/")]
                     if name[0] in "qx":
                         piece = (name[0], at[name[1:] or "i"])
@@ -99,7 +179,7 @@ def plan(T, topo):
                         piece = ("v", keys if name == "v" else (home if name[1] == "C" else far)[at[name[2]]])
                     else:
                         piece = (name,)
-                    calls[c].append((piece, ways))
+                    calls[c].append((piece, ways, slice(int(part), int(part) + 1) if part else slice(None), text[0] == "&"))
     return cores, calls, role
 
 
@@ -107,19 +187,36 @@ def slot(i, me):
     return 2 - (i - me) % 3
 
 
-def pieces(piece, me, there):
-    n, later, there = piece[0], there[0] == "rank", there[2]
+def moving(role):
+    return (0, TQ, 3 * TQ, 2 * TQ) if role[0] == "rank" else (TQ, 2 * TQ, 3 * TQ, 0)
+
+
+def pieces(piece, here, there):
+    ca, cb = moving(here), moving(there)
+    n, later, me, there = piece[0], there[0] == "rank", here[2], there[2]
+    if n == "rx":
+        return "rx", [(b, b, ca[3], cb[3], 2 * TQ) for b in ("mc", "mp")]
     if n == "kp":
         return "kp", [("kpi", "kpi", 0, 4 * later, 4)]
+    if n[:2] == "ta":
+        return "t" + n[2], [(b, b, 0, 896 + 128 * int(n[2]), 128) for b in ("kc",)]
+    if n[:2] == "tb":
+        return "kc0", [(b, b, 896 + 128 * int(n[2]), 0, 128) for b in ("kc",)]
+    if n == "kf":
+        return "kfs", [("kf", "kf", 0, 4 * later, 4)]
+    if n == "kg":
+        return "kgs", [("kf", "kf", 0, 4, 4)]
+    if n in ("og", "oh"):
+        return "og", [("og", "og", 64 * (n == "oh"), 0, 64)]
     if n == "q":
         return "q%d" % piece[1], [("qpi", "qpi", 16 * slot(piece[1], me), 16 * slot(piece[1], there), 16)]
     if n[:2] in ("kc", "ks", "kk"):
         a, e = 128 * int(n[2]), 128 * int(n[3])
         return n[:3], [(b, b, a, a + 512 * later, e - a) for b in (("kc", "ks") if n[1] == "k" else (n[:2],))]
     if n == "r":
-        return "r", [("rc", "rc", 0, 0, TQ), ("rp", "rp", 0, 0, TQ)]
+        return "r", [(b, b, ca[3], cb[3], TQ) for b in ("mc", "mp")]
     if n == "x":
-        return "x%d" % piece[1], [(b, b, TQ * slot(piece[1], me), TQ * slot(piece[1], there), TQ) for b in ("xc", "xp")]
+        return "x%d" % piece[1], [(b, b, ca[slot(piece[1], me)], cb[slot(piece[1], there)], TQ) for b in ("mc", "mp")]
     if n == "v":
         return "v%d" % piece[1], [(b, b, 128 * piece[1], 128 * piece[1], 128) for b in ("vc", "vp")]
     s, u0, u1 = piece[1:]
@@ -134,8 +231,9 @@ def rank_program(g, core, T, topo):
     place = [(me + 2) % 3, (me + 1) % 3, me]
     due, block = {}, {}
     for c in calls:
-        for piece, ways in calls[c]:
-            sem, parts = pieces(piece, 0, role[core])
+        for piece, ways, part, _ in calls[c]:
+            sem, parts = pieces(piece, role[c], role[core])
+            parts = parts[part]
             for es, ds in ways:
                 if core in ds:
                     due[sem] = due.get(sem, 0) + len(es) * len(parts)
@@ -149,6 +247,13 @@ def rank_program(g, core, T, topo):
     count, seen, sent = {"v": 0, "s": 0, "t": 0}, {}, [0]
     at = {sem: (sem, due[sem]) for sem in due}
     rank = kind == "rank"
+    if "kfs" in due:
+        at["kf", int(rank)] = at["kfs"]
+    if "kgs" in due:
+        at["kf", 1] = at["kgs"]
+    if "rx" in due:
+        at["r"] = at["x%d" % place[0]] = at["rx"]
+    col = moving(role[core])
 
     def after(q, deps):
         for d in deps:
@@ -167,32 +272,45 @@ def rank_program(g, core, T, topo):
     def step(q, s):
         n = s[0]
         if q == "g":
-            piece, ways = s
-            sem, parts = pieces(piece, me, role[core])
+            def transfers(k):
+                for piece, ways, part, _ in s:
+                    sem, parts = pieces(piece, role[core], role[core])
+                    a, b, ca, _, w = parts[part][k]
+                    for es, ds in ways:
+                        sent[0] += len(es)
+                        yield RemoteDMATransfer(
+                            dst_ids=[DstId(rid=topo.addr(d)[0], pnc=topo.addr(d)[1]) for d in ds], dma_engine_mask=sum(1 << e for e in es),
+                            remote_sem=T.sem[sem], srcs=[view(a, ca, w)], dsts=[view(b, pieces(piece, role[core], role[d])[1][part][k][3], w) for d in ds])
 
             def call():
-                for k, (a, b, ca, _, w) in enumerate(parts):
-                    g.remote_dma_fused([RemoteDMATransfer(
-                        dst_ids=[DstId(rid=topo.addr(d)[0], pnc=topo.addr(d)[1]) for d in ds], dma_engine_mask=sum(1 << e for e in es),
-                        remote_sem=T.sem[sem], srcs=[view(a, ca, w)], dsts=[view(b, pieces(piece, me, role[d])[1][k][3], w) for d in ds])
-                        for es, ds in ways], local_sem=T.sem.sent)
-                    sent[0] += sum(len(es) for es, _ in ways)
-            if piece[0][:2] in ("kc", "ks", "kk"):
-                return [d for a, _, ca, _, w in parts for b in range(ca // 128, (ca + w) // 128) for d in block[a, b]], call, []
-            if piece[0] == "kp" and rank:
-                return ["l_p"], call, []
-            return [("Z", u) for u in range(piece[2], piece[3])] if piece[0] == "a" else [sem], call, []
+                for k in range(len(pieces(s[0][0], role[core], role[core])[1][s[0][2]])):
+                    g.remote_dma_fused(list(transfers(k)), local_sem=T.sem.sent)
+
+            def needs(piece):
+                sem, parts = pieces(piece, role[core], role[core])
+                if piece[0][:2] in ("kc", "ks", "kk", "ta", "tb"):
+                    return [d for a, _, ca, _, w in parts for b in range(ca // 128, (ca + w) // 128) for d in block[a, b]]
+                if piece[0] == "a":
+                    return [("Z", u) for u in range(piece[2], piece[3])]
+                return {"rx": ["r", "x%d" % me], "kf": [("kf", 0)], "kg": [("kf", 0)], "oh": ["oh"], "kp": ["l_p" if rank else "kp"]}.get(piece[0], [sem])
+            return [d for x in s for d in needs(x[0])], call, []
         if n == "Q":
             if s[1] == "k":
                 a, e = 128 * int(s[2]), 128 * int(s[3])
                 return ["l_" + s[1:3]], lambda: g.vector.quantize_mx(T.kc[:, a:e], T.ks[:, a:e], T.kt[:, 4 * a:4 * e]), [s[1:]]
-            name, c, p, a, src = {"r": ("r", "rc", "rp", 0, T.rtt[:]), "x": ("x%d" % me, "xc", "xp", 2 * TQ, T.xt[:]),
+            name, c, p, a, src = {"r": ("r", "mc", "mp", col[3], T.rtt[:]), "x": ("x%d" % me, "mc", "mp", col[2], T.xt[:]),
                                   "v": ("v%d" % keys, "vc", "vp", 128 * keys, T.vt[:])}[s[1:]]
             w = src.shape[1] // 4
             return ["l_" + s[1:]], lambda: g.vector.quantize_mx(T[c][:, a:a + w], T[p][:, a:a + w], src), [name]
         if n == "C":
             a = 32 * int(s[1])
-            return ["l_q"], lambda: g.vector.tensor_copy(T.qpi[a:a + 32, 32:48], T.qpi[0:32, 32:48]), ["q%d" % me]
+            return ["l_q"], lambda: g.vector.tensor_copy(T.qpi[a:a + 32, 32:48], T.qld[0:32, :]), ["q%d" % me]
+        if n == "h":
+            b = int(s[1])
+            a = 0 if b // 4 else 32
+            return ([("kf", b // 4), "q%d" % place[a // 16]],
+                    lambda: g.vector.tensor_scalar(T.og[:, 16 * b:16 * b + 16], T.qpi[:, a:a + 16], T.kf[:, b:b + 1], 255.0, SUB, MIN),
+                    {3: ["og"], 7: ["oh"]}.get(b, []))
         if n == "F":
             a = int(s[1])
             return (["l_p" if rank and not a else "kp"], lambda: g.vector.tensor_scalar(T.kf[:, a:a + 4], T.kpi[:, a:a + 4], 128.0, None, SUB),
@@ -208,10 +326,10 @@ def rank_program(g, core, T, topo):
             k = turn[0] % banks
             deps = block["kc", b] + block["ks", b] + users[k]
             if n == "P":
-                deps, c, p, a, w, drains = deps + ["r"], "rc", "rp", 0, TQ, [("W", b)]
+                deps, a, m, w, drains = deps + ["r"], 0, col[3], TQ, [("W", b)]
             else:
                 us = range(*SPAN[s[1]])
-                deps, c, p, a, w = deps + ["x%d" % place[u // 2] for u in us], "xc", "xp", U * us[0], U * len(us)
+                deps, a, m, w = deps + ["x%d" % place[u // 2] for u in us], U * us[0], col[us[0] // 2] + U * (us[0] % 2), U * len(us)
                 drains = [("A", b, u) for u in us]
 
             def call():
@@ -220,7 +338,7 @@ def rank_program(g, core, T, topo):
                 for d in drains:
                     bank[d] = (k, a)
                 return g.tensor.matmul_mx(T["ps%d" % k][:, 0:w], T.kc[:, 128 * b:128 * b + 128], T.ks[:, 128 * b:128 * b + 128],
-                                          T[c][:, a:a + w], T[p][:, a:a + w], True, True)
+                                          T.mc[:, m:m + w], T.mp[:, m:m + w], True, True)
             return deps, call, [("mm",) + d for d in drains]
         if n == "W":
             b = int(s[1])
@@ -235,7 +353,8 @@ def rank_program(g, core, T, topo):
                     lambda: g.tensor.matmul_mx(T.ps7[:, 0:TQ], T.vc[:, 128 * r:128 * r + 128], T.vp[:, 128 * r:128 * r + 128],
                                                T.ac[:, TQ * r:TQ * r + TQ], T.ap[:, TQ * r:TQ * r + TQ], start, stop), ["y"] if stop else [])
         if n == "O":
-            return ["y"], lambda: g.scalar.activation(T.ys[:], T.ps7[:, 0:TQ], COPY), ["out"]
+            return (["y"], lambda: g.vector.tensor_copy(T.ys[:], T.ps7[:, 0:TQ]) if q == "v" else g.scalar.activation(T.ys[:], T.ps7[:, 0:TQ], COPY),
+                    ["out"])
         u0, u1 = SPAN[s[1]]
         us = range(u0, u1)
         b = int(s[2])
@@ -248,11 +367,13 @@ def rank_program(g, core, T, topo):
                     lambda: g.vector.quantize_mx(T[c][:, a:a + w], T[p][:, a:a + w], T.ht[:, h0 + 4 * U * u0:h0 + 4 * U * u1]),
                     [("Z", u + 6 * (b // 4)) for u in us])
         if n == "G":
+            given = b >= 4 and "og" in due
+            li = T.og[:, 16 * (b - 6) + 8 * u0:16 * (b - 6) + 8 * u1] if given else T.of[:, 48 * b + 8 * u0:48 * b + 8 * u1]
 
             def call():
-                o, w = T.gg[:, 768 * b + U * u0:768 * b + U * u1], T.pw[:, TQ * b:TQ * b + TQ].indirect(T.of[:, 48 * b + 8 * u0:48 * b + 8 * u1])
+                o, w = T.gg[:, 768 * b + U * u0:768 * b + U * u1], T.pw[:, TQ * b:TQ * b + TQ].indirect(li)
                 return g.vector.tensor_copy(o, w) if q == "v" else g.scalar.activation(o, w, COPY)
-            return [("W", b)] + [("of", b, u) for u in us], call, [("G", b, u) for u in us]
+            return [("W", b)] + (["og"] if given else [("of", b, u) for u in us]), call, [("G", b, u) for u in us]
         if n == "A":
 
             def call():
@@ -289,11 +410,16 @@ def rank_program(g, core, T, topo):
     def cfg(q):
         out = []
         for s in CFG.get("%s%d.%s" % (kind, idx, q), CFG.get(kind + "." + q)).split():
-            out += ["l%s%d" % (s[1], int(s[2]) + b) for b in B] if s[0] == "L" else [s]
+            out += ["l%s%d" % (s[1], int(s[2]) + b) for b in B] if s[0] == "L" else ["h%d" % (b + 4 * (s == "J")) for b in B] if s in "HJ" else [s]
         return out
 
     queues = {q: cfg(q) for q in "vst"}
-    queues["g"] = list(calls[core])
+    queues["g"] = []
+    for x in calls[core]:
+        if x[3]:
+            queues["g"][-1].append(x)
+        else:
+            queues["g"].append([x])
     if rank:
         for s in queues["v"]:
             if s[0] == "Z" and SPAN[s[1]][0] >= 4:
@@ -303,9 +429,12 @@ def rank_program(g, core, T, topo):
                     block["kc", b] = block["ks", b] = [s[1:]]
         g.sync.dma_start(T.kpi[:, 0:4], T.kp[:]).then_inc(T.sem.l_p, 16)
         for k in range(2):
-            g.scalar.dma_start(T.qpi[16 * k:16 * k + 16, 32:48], T.qp[:]).then_inc(T.sem.l_q, 16)
+            g.scalar.dma_start(T.qld[16 * k:16 * k + 16, :], T.qp[:]).then_inc(T.sem.l_q, 16)
         src = {"r": (T.rtt[:], T.rt[:]), "x": (T.xt[:], T.qx[:]), "v": (T.vt[:], T.vv[:])}
         for n in CFG.get("loads%d" % me, CFG["loads"]).split():
+            if n[0] == "~":
+                after("y", [at["l_" + n[1:]]])
+                continue
             if n[0] == "k":
                 a, e = 512 * int(n[1]), 512 * int(n[2])
                 src[n] = (T.kt[:, a:e], T.ky[:, a:e])
@@ -316,8 +445,9 @@ def rank_program(g, core, T, topo):
         ys = [("Y", r, r == order[0], r == order[-1]) for r in order]
         queues["t"] = [ys.pop(0) if s == "Y" else s for s in queues["t"]] + ys
         run(queues)
-        after("s", [at["out"]])
-        g.scalar.dma_start(T.y[:], T.ys[:]).then_inc(T.sem.stored, 16)
+        last = "s" if at["out"][0] == "ss" else "y"
+        after(last, [at["out"]])
+        eng[last].dma_start(T.y[:], T.ys[:]).then_inc(T.sem.stored, 16)
         after("g", [("stored", 16)])
     else:
         run(queues)

from concourse.bass import DstId, RemoteDMATransfer
from concourse.mybir import dt, AluOpType, ActivationFunctionType

NR, TQ, U = 6, 256, 128
F8 = "float8_e4m3fn_x4"
SCRATCH = {
    "kt": ("sbuf", [128, 2048], "bfloat16"),
    "xt": ("sbuf", [128, 1024], "bfloat16"),
    "rtt": ("sbuf", [128, 1024], "bfloat16"),
    "vt": ("sbuf", [128, 512], "bfloat16"),
    "mc": ("sbuf", [128, 4 * TQ], F8), "mp": ("sbuf", [128, 4 * TQ], "uint8"),
    "kc": ("sbuf", [128, 1280], F8), "ks": ("sbuf", [128, 1280], "uint8"),
    "kpi": ("sbuf", [128, 8], "int32"), "kf": ("sbuf", [128, 8], "float32"),
    "qld": ("sbuf", [128, 16], "int32"), "qpi": ("sbuf", [128, 48], "uint16"),
    "og": ("sbuf", [128, 128], "uint16"),
    "of": ("sbuf", [128, 8 * 48], "uint16"),
    "pw": ("sbuf", [128, 8 * TQ], "float32"),
    "gg": ("sbuf", [128, 24 * TQ], "float32"),
    "ht": ("sbuf", [128, 24 * TQ], "bfloat16"),
    "oc": ("sbuf", [128, 3 * TQ], F8), "op": ("sbuf", [128, 3 * TQ], "uint8"),
    "vc": ("sbuf", [128, NR * 128], F8), "vp": ("sbuf", [128, NR * 128], "uint8"),
    "ac": ("sbuf", [128, NR * TQ], F8), "ap": ("sbuf", [128, NR * TQ], "uint8"),
    "ys": ("sbuf", [128, TQ], "float32"),
}
for _i in range(8):
    SCRATCH["ps%d" % _i] = ("psum", [128, 512], "float32")

SEMAPHORES = (["l_p", "l_q", "l_v", "l_r", "l_x", "vs", "ss", "ts", "sent", "stored", "kp", "r", "og", "t1", "t2", "kfs", "kgs", "rx"]
              + ["%s%d" % (n, i) for n in ("kc", "ks", "kk", "l_k") for i in range(4)]
              + ["%s%d" % (n, i) for n in "qx" for i in range(3)] + ["%s%d" % (n, i) for n in "va" for i in range(NR)])
SPAN = {"p": (0, 2), "n": (2, 4), "i": (4, 6), "w": (0, 4), "z": (2, 6), "a": (0, 6),
        "0": (0, 1), "1": (1, 2), "2": (2, 3), "3": (3, 4), "4": (4, 5), "5": (5, 6)}
CFG = {
    "loads": "k02 x r k24 v",
    "rank.g": "kp OFF A; q ON Fn Cn Cp Fp; kk02 OFF A; x ON Fn; r ON Fi; x ON Cn; kk24 OFF A; x ON Fp / OFF Cp; v OFF A / ON Cn Cp; ap ALL Cp; an ALL Cn",
    "first.g": "kp ALL Ci; kk02 ALL Ci; kk24 ALL Ci; v ALL C0 C1 C2; ap ALL Cp; an ALL Cn",
    "rank.v": "C1 C2 C3 F0 Qk02 Li0 Qx Qr Qk24 Qv W2 W3 Ai0 Lw0 Ai1 Ai2 Ai3 Ri01 Zi0 Ap0 Ap1 Ap2 Ap3 F4 Rp01 Li4 Zp0 An0 An1 An2 An3 Rn01 Zn0 Ai4 Ai5 Ai6 Ai7 Ri64 Ri74 Zi4",
    "rank.s": "W0 W1 Gi0 Gi1 Gi2 Gi3 Gp0 Gp1 Gp2 Gp3 Gn0 Gn1 Gn2 Gn3 W4 W5 Gi4 Gi5 W6 W7 Gi6 Gi7 Ri44 Ri54 O01",
    "rank.t": "P0 P1 P2 P3 Si0 Si1 Si2 Si3 Sp0 Sp1 Sp2 Sp3 Sn0 Sn1 P4 P5 Sn2 Sn3 Si4 Si5 P6 P7 Si6 Si7",
    "rank.y": "Ci Cn Fn Cp Fi Fp",
    "first.v": "F0 Lw0 W1 Ap0 Ap1 An0 Rw04 An1 W3 Rw14 Ap2 Rp24 Ap3 Rp34 Zp0 An2 An3 Rn24 Rn34 Zn0",
    "first.s": "W0 Gp0 Gp1 Gn0 Gn1 W2 Gp2 Gp3 Gn2 Gn3",
    "first.t": "P0 P1 Sp0 Sp1 Sn0 Sn1 P2 P3 Sp2 Sp3 Sn2 Sn3",
}
CFG["rank.v"] = "C0 " + CFG["rank.v"]
CFG.update({
    "rank.g": "kp OFF A; q ON Fn Cn Cp Fp; kk02 OFF A; x ON Fn; r ON Fi; x ON Cn; ks24 OFF A; kc23 OFF A; kc34 OFF A; x ON Fp / OFF Cp; v OFF A / ON Cn Cp; ap ALL Cp; an ALL Cn",
    "first.t": "P0 P1 Sp0 Sp1 Sn0 Sn1 P2 Sp2 Sn2 P3 Sp3 Sn3",
    "first.s": "W0 Gp0 Gp1 Gn0 Gn1 W2 Gp2 Gn2 W3 Gp3 Gn3",
    "first.v": "F0 Lw0 W1 Ap0 Ap1 An0 Rw04 An1 Rw14 Ap2 An2 Rw24 Ap3 Rp34 Zp0 An3 Rn34 Zn0",
})
CFG.update({
    "loads": "k02 r x k24 v",
    "rank.g": "kp OFF A; q ON Fn Cn Cp Fp; kc01 OFF A; r ON Fi; x ON Fn; ks04 OFF A; kc12 OFF A; x ON Cn; kc23 OFF A; kc34 OFF A; x ON Cp; v OFF A / ON Cn Cp; ap ALL Cp; an ALL Cn",
    "first.g": "kf ALL Ci; xp ALL Fn; kc02 ALL Ci; ks04 ALL Ci; kc23 ALL Ci; kc34 ALL Ci; v ALL C0 C1 C2; ap ALL Cp; an ALL Cn",
    "first.v": "F0 Lw0 Gn0 Ap0 Rp04 Gn1 Ap1 Rp14 An1 An0 An2 Ap2 Rn14 Rp24 Ap3 Rn24 An3 Rn04 Zp0 Zn0",
    "first.s": "W0 Gp0 W1 Gp1 W2 Gn2 Gp2 W3 Gp3 Gn3 Rp34 Rn34",
    "first.t": "P0 Sp0 P1 Sp1 P2 Sn0 Sn1 Sn2 Sn3 P3 Sp2 Sp3",
    "rank.v": "C0 C1 C2 C3 F0 Qk02 Li0 Qr Qx Qk24 Qv Gi0 Ai0 Lw0 Gp0 Ai1 Ai2 Gn3 Gp2 Ai3 Gn0 Li4 Ap3 Ap1 Ap0 Ap2 An0 Rp02 An2 An3 An1 Rn02 Rn12 Zp0 Zn0 Zi0 Ai4 Ai6 Ai7 Ai5 Ri54 Zi4",
    "rank.s": "W0 W1 W2 Gi1 W3 Gi2 Gn2 Gi3 Gp1 Ri02 Gp3 Gn1 Ri12 Rp12 W4 W5 W6 Gi4 Gi5 W7 Gi6 Gi7 Ri44 Ri64 Ri74 O01",
    "rank.t": "P0 P1 Si0 P2 Si1 P3 Si2 Si3 Sp3 Sp1 Sp0 Sp2 Sn3 Sn0 P4 Sn2 P5 P6 Sn1 P7 Si4 Si6 Si5 Si7",
    "rank.y": "Ci Cn Fn Cp Fi Fp",
})
CFG.update({
    "first0.g": "kf ALL Ci; xp ALL Fn; kc02 ALL Ci; ks04 ALL Ci; kc24 ALL Ci; v ALL C0 C1 C2; ap ALL Cp; an ALL Cn",
    "first.g": "kf ALL Ci; xp ALL Fn; ks04 ALL Ci; kc13 ALL Ci; kc01 ALL Ci; kc34 ALL Ci; v ALL C0 C1 C2; ap ALL Cp; an ALL Cn",
    "rank0.g": "kp OFF A; q ON Fn Cn Cp Fp; kc02 OFF A; rx ON Fn; ks04 OFF A; x ON Cn; kc24 OFF A; x ON Cp; tb1 OFF A1; tb2 OFF A2; v OFF A / ON Cn Cp; ap ALL Cp; an ALL Cn",
    "rank1.g": "kp OFF A; q ON Fn Cn Cp Fp; kc12 LO A; ta1 HI C0; rx ON Fn; ks04 OFF A; x ON Cn; kc23 OFF A; kc34 OFF A; x ON Cp; v OFF A / ON Cn Cp; ap ALL Cp; an ALL Cn",
    "rank2.g": "kp OFF A; q ON Fn Cn Cp Fp; kc12 LO A; ta2 HI C0; rx ON Fn; ks04 OFF A; x ON Cn; kc23 OFF A; kc34 OFF A; x ON Cp; v OFF A / ON Cn Cp; ap ALL Cp; an ALL Cn",
    "first.v": "F0 Lw0 W1 Gp1 Ap1 Rp14 Gn2 Ap2 Gp0 An2 Ap0 An1 An0 Ap3 Rp04 Rn14 An3 Zp0 Rn24 Zn0",
    "first.s": "Gn1 W2 Gp2 W0 W3 Gn0 Gp3 Rp24 Gn3 Rp34 Rn04 Rn34",
    "first.t": "P1 Sp1 P2 Sp2 P0 P3 Sn1 Sn2 Sp0 Sp3 Sn3 Sn0",
    "first0.v": "F0 Lw0 W1 W2 W3 Gw1 Ap0 Ap1 Ap2 Ap3 An0 An2 An1 An3 Zp0 Rn12 Zn0",
    "first0.s": "W0 Gw0 Gw2 Gw3 Rp01 Rn02",
    "first0.t": "P0 P1 P2 P3 Sp2 Sp3 Sp1 Sp0 Sn2 Sn0 Sn3 Sn1",
    "rank.v": "C0 C1 C2 C3 F0 Qk02 Li0 Qr Qx Qk24 Qv Gi1 Ai1 Gi2 Lw0 Ai2 Ai0 Ai3 Gw2 Li4 Ap0 Ap1 Ap2 Ap3 An1 An2 An0 An3 Zp0 Rn01 Zi0 Zn0 Gi7 Ai6 Ai7 Ai5 Ai4 Ri42 Zi4",
    "rank.s": "W1 W0 W2 W3 Gi0 Gi3 Gw1 Gw0 Gw3 Ri01 Rp01 W5 W6 W7 Gi6 W4 Gi5 Gi4 Ri52 O01",
    "rank.t": "P1 P0 P2 Si1 P3 Si0 Si3 Si2 Sp0 Sp1 Sp2 Sp3 Sn1 Sn2 Sn0 P5 Sn3 P6 P7 Si5 Si6 Si7 Si4 P4",
    "rank.y": "Ci Cn Cp Fn Fi Fp",
})
for _k in list(CFG):
    if _k.endswith(".g"):
        CFG[_k] = CFG[_k].replace("q ON Fn Cn Cp Fp", "q ON Fn Cn Cp Fi").replace("kf ALL Ci; xp ALL Fn", "qp ALL Fn; xp ALL Fn; og ALL Ci")
CFG.update({
    "first.v": "F0 Lp0 H Ln0 Gn1 Ap1 Rp14 Gp2 An1 Ap2 An2 Gp3 Ap0 Ap3 Rp04 Rp24 An3 An0 Zp0 Rn04 Zn0",
    "first.s": "W1 Gp1 W2 Gn2 W0 W3 Gp0 Gn0 Gn3 Rp34 Rn24 Rn34 Rn14",
    "first.t": "P1 Sp1 P2 Sp2 P0 Sn1 P3 Sn2 Sp0 Sn3 Sp3 Sn0",
    "first0.v": "F0 Lp0 H Ln0 W1 W2 W3 Gw1 Ap0 Ap1 Ap2 Ap3 An0 An2 An1 An3 Zp0 Rn12 Zn0",
    "rank.v": "C0 C1 C2 C3 Qk02 Qr F0 Qx li1 Qk24 Qv li0 li2 li3 W2 Ai1 Lw0 Gi3 Ai0 Gw2 Ai3 Ai2 Ap0 Ap2 Ap1 Ap3 An3 An0 An2 An1 Zi0 Zp0 Rn01 Zn0 Gi7 Ai5 Ai7 Ai4 Ai6 Ri42 Zi4",
    "rank.s": "W1 W0 Gi1 W3 Gi0 Gi2 Gw0 Gw3 Gw1 Ri01 Rp01 W5 W4 W7 Gi5 W6 Gi4 Gi6 Ri52 O01",
    "rank.t": "P1 P0 P2 P3 Si1 Si2 Si0 Si3 Sp0 Sp2 Sp1 Sp3 Sn3 Sn2 Sn0 Sn1 P4 P5 Si6 Si7 P7 Si5 P6 Si4",
})
for _k in list(CFG):
    if _k.endswith(".g"):
        CFG[_k] = (CFG[_k].replace("q ON Fn Cn Cp Fi", "q ON Fn Cn Cp").replace("qp ALL Fn;", "qp ALL Fn Fp;")
                   .replace("og ALL Ci; ks04 ALL Ci; kc13 ALL Ci;", "ks04 ALL Ci; kc13 ALL Ci; og ALL Ci;")
                   .replace("og ALL Ci; kc02 ALL Ci; ks04 ALL Ci; kc24 ALL Ci", "kc02 ALL Ci; ks04 ALL Ci; kc24 ALL Ci; og ALL Ci"))
    if _k.endswith(".v"):
        CFG[_k] = CFG[_k].replace("Lp0 H Ln0", "Lp0 Ln0 H")
CFG.update({
    "rank.v": "C0 C1 C2 C3 F0 Qk02 Li0 Qr Qx Qk24 Qv Gi0 Lw0 Gw0 Ai2 Ai0 Gw2 Ai1 Ai3 Ap3 Ap0 Ap2 Ap1 An0 An3 An1 An2 Zp0 Rn01 Zi0 Zn0 Gi7 Ai5 Ai7 Ai4 Ai6 Ri42 Zi4",
    "rank.s": "W0 W1 W2 W3 Gi2 Gi1 Gw3 Gi3 Gw1 Ri01 Rp01 W6 W5 W7 W4 Gi5 Gi4 Gi6 Ri52 O01",
    "rank.t": "P0 P1 P2 P3 Si0 Si2 Si1 Si3 Sp3 Sp0 Sp2 Sp1 Sn0 Sn2 Sn3 Sn1 P6 P5 Si5 P7 Si6 P4 Si7 Si4",
})
CFG.update({
    "rank.v": "C0 C1 C2 C3 F0 Qk02 Li0 Qr Qx Qk24 Qv Gi0 Ai0 Lw0 Gw0 Ai1 Ai2 Gw2 Ai3 Ap0 Ap2 Ap3 Ap1 An0 Rp01 An2 Zp0 An3 An1 Rn01 Zn0 Zi0 Ai5 Ai6 Ai4 Ai7 Ri52 Zi4",
    "rank.s": "W0 W1 W2 W3 Gi1 Gi2 Gi3 Gw3 Gw1 Ri01 W5 W6 Gi5 Gi6 W4 Gi4 W7 Gi7 Ri42 O01",
    "rank.t": "P0 P1 Si0 P2 P3 Si1 Si2 Si3 Sp0 Sp2 Sp3 Sp1 Sn0 Sn2 P5 P6 Sn3 Sn1 P4 P7 Si5 Si6 Si4 Si7",
})
CFG.update({
    "first0.g": "qp ALL Fn X2; kg ALL X1; xp ALL Fn; kc02 ALL Ci; ks04 ALL Ci; kc24 ALL Ci; v ALL C0 C1 C2; ap ALL Cp; an ALL Cn",
    "first1.g": "qp ALL Fn X1; kf ALL X1; xp ALL Fn; ks04 ALL Ci; kc13 ALL Ci; kc01 ALL Ci; kc34 ALL Ci; v ALL C0 C1 C2; ap ALL Cp; an ALL Cn",
    "first2.g": "qp ALL Fn X1; kf ALL X2; xp ALL Fn; ks04 ALL Ci; kc13 ALL Ci; kc01 ALL Ci; kc34 ALL Ci; v ALL C0 C1 C2; ap ALL Cp; an ALL Cn",
    "second1.g": "og ON C1; oh ON C0", "second2.g": "og ON C2",
    "second1.v": "H J", "second2.v": "H", "second.s": "", "second.t": "",
    "first.v": "F0 Lp0 Ln0 Gn1 Ap1 Rp14 Gp2 An1 Ap2 An2 Gp3 Ap0 Ap3 Rp04 Rp24 An3 An0 Zp0 Rn04 Zn0",
    "first0.v": "F0 Lp0 Ln0 W1 W2 W3 Gw1 Ap0 Ap1 Ap2 Ap3 An0 An2 An1 An3 Zp0 Rn12 Zn0",
})
CFG.update({
    "first0.v": "F0 Lp0 Ln0 Gn1 Gp0 Gp3 Ap0 Ap1 Ap3 An1 Ap2 An3 Rp12 An0 An2 Zp0 Rn02 Zn0",
    "first0.s": "W1 W0 W3 W2 Gp1 Gp2 Gn3 Gn0 Gn2 Rp02 Rn12",
    "first0.t": "P1 P0 P3 P2 Sp0 Sp1 Sp3 Sn1 Sp2 Sn3 Sn0 Sn2",
})


def layout(T, topo):
    cores = list(T.cores)
    sides = []
    for chip in sorted({topo.chip(c) for c in cores}):
        ranks = [q for q in range(NR) if topo.chip(cores[q]) == chip]
        ranks.sort(key=lambda q: sum(topo.die(cores[p]) == topo.die(cores[q]) for p in ranks))
        sides.append(ranks)
    first, second = {}, {}
    for k in range(2):
        idle = [c for c in topo.cores_of(cores[sides[k][0]]) if c not in cores]
        for s in sides[1 - k]:
            idle.sort(key=lambda c: (topo.die(c) != topo.die(cores[s]), -c))
            first[s] = idle.pop(0)
        for s in sides[1 - k][1:]:
            second[s] = idle.pop(0)
    return cores, sides, first, second


def plan(T, topo):
    cores, sides, first, second = layout(T, topo)
    ALL = topo.engines(cores[sides[0][0]], cores[sides[0][1]])
    OFF = topo.engines(cores[sides[0][0]], cores[sides[1][0]])
    ON = [e for e in ALL if e not in OFF]
    h = len(OFF) // 2
    E = {"ALL": ALL, "OFF": OFF, "ON": ON, "LO": OFF[:h], "HI": OFF[h:], "EV": OFF[::2], "OD": OFF[1::2], "ON1": ON[:h], "ON2": ON[h:]}
    calls, role = {}, {}
    for k in range(2):
        home, far = sides[k], sides[1 - k]
        for i, r in enumerate(home):
            at = {"i": i, "n": (i + 1) % 3, "p": (i + 2) % 3, "0": 0, "1": 1, "2": 2}
            who = {"A": first[r]}
            for a, j in at.items():
                who["C" + a], who["F" + a], who["X" + a] = cores[home[j]], first[far[j]], second.get(far[j])
                who["A" + a], who["B" + a], who["M" + a] = first[home[j]], second.get(home[j]), cores[far[j]]
            for kind, c, keys in (("rank", who["Ci"], r), ("first", who["Fi"], far[i]), ("second", who["Xi"], far[i])):
                text = CFG.get("%s%d.g" % (kind, i), CFG.get(kind + ".g"))
                if c is None or text is None:
                    continue
                me = i
                if kind == "second":
                    w = CFG.get("second%d.keys" % i, "Fi")
                    keys, me = (home if w[0] == "C" else far)[at[w[1]]], at[w[1]]
                role[c] = (kind, keys, me, home, far, i)
                calls[c] = []
                for text in filter(None, text.replace("&", ";&").split(";")):
                    name, rest = text.strip("&").split(None, 1)
                    name, _, part = name.partition(".")
                    ways = [(E[w.split()[0]], [who[d] for d in w.split()[1:]]) for w in rest.split("/")]
                    if name[0] in "qx":
                        piece = (name[0], at[name[1:] or "i"])
                    elif name[0] == "a":
                        piece = ("a", keys) + SPAN[name[1]]
                    elif name[0] == "v":
                        piece = ("v", keys if name == "v" else (home if name[1] == "C" else far)[at[name[2]]])
                    else:
                        piece = (name,)
                    calls[c].append((piece, ways, slice(int(part), int(part) + 1) if part else slice(None), text[0] == "&"))
    return cores, calls, role


def slot(i, me):
    return 2 - (i - me) % 3


def moving(role):
    return (0, TQ, 3 * TQ, 2 * TQ) if role[0] == "rank" else (TQ, 2 * TQ, 3 * TQ, 0)


def pieces(piece, here, there):
    ca, cb = moving(here), moving(there)
    n, later, me, there = piece[0], there[0] == "rank", here[2], there[2]
    if n == "rx":
        return "rx", [(b, b, ca[3], cb[3], 2 * TQ) for b in ("mc", "mp")]
    if n == "kp":
        return "kp", [("kpi", "kpi", 0, 4 * later, 4)]
    if n[:2] == "ta":
        return "t" + n[2], [(b, b, 0, 896 + 128 * int(n[2]), 128) for b in ("kc",)]
    if n[:2] == "tb":
        return "kc0", [(b, b, 896 + 128 * int(n[2]), 0, 128) for b in ("kc",)]
    if n == "kf":
        return "kfs", [("kf", "kf", 0, 4 * later, 4)]
    if n == "kg":
        return "kgs", [("kf", "kf", 0, 4, 4)]
    if n in ("og", "oh"):
        return "og", [("og", "og", 64 * (n == "oh"), 0, 64)]
    if n == "q":
        return "q%d" % piece[1], [("qpi", "qpi", 16 * slot(piece[1], me), 16 * slot(piece[1], there), 16)]
    if n[:2] in ("kc", "ks", "kk"):
        a, e = 128 * int(n[2]), 128 * int(n[3])
        return n[:3], [(b, b, a, a + 512 * later, e - a) for b in (("kc", "ks") if n[1] == "k" else (n[:2],))]
    if n == "r":
        return "r", [(b, b, ca[3], cb[3], TQ) for b in ("mc", "mp")]
    if n == "x":
        return "x%d" % piece[1], [(b, b, ca[slot(piece[1], me)], cb[slot(piece[1], there)], TQ) for b in ("mc", "mp")]
    if n == "v":
        return "v%d" % piece[1], [(b, b, 128 * piece[1], 128 * piece[1], 128) for b in ("vc", "vp")]
    s, u0, u1 = piece[1:]
    return "a%d" % s, [(a, b, U * u0, TQ * s + U * (u0 % 2), U * (u1 - u0)) for a, b in (("oc", "ac"), ("op", "ap"))]


def rank_program(g, core, T, topo):
    cores, calls, role = plan(T, topo)
    if core not in role:
        return
    kind, keys, me, home, far, idx = role[core]
    place = [(me + 2) % 3, (me + 1) % 3, me]
    due, block = {}, {}
    for c in calls:
        for piece, ways, part, _ in calls[c]:
            sem, parts = pieces(piece, role[c], role[core])
            parts = parts[part]
            for es, ds in ways:
                if core in ds:
                    due[sem] = due.get(sem, 0) + len(es) * len(parts)
                    for a, _, _, ca, w in parts:
                        if a in ("kc", "ks"):
                            for b in range(ca // 128, (ca + w) // 128):
                                block[a, b] = [sem]
    ADD, MAX, MIN, MULT, SUB = AluOpType.add, AluOpType.max, AluOpType.min, AluOpType.mult, AluOpType.subtract
    COPY, RELU = ActivationFunctionType.Copy, ActivationFunctionType.Relu
    eng = {"g": g, "v": g.vector, "s": g.scalar, "t": g.tensor, "y": g.sync}
    count, seen, sent = {"v": 0, "s": 0, "t": 0}, {}, [0]
    at = {sem: (sem, due[sem]) for sem in due}
    rank = kind == "rank"
    if "kfs" in due:
        at["kf", int(rank)] = at["kfs"]
    if "kgs" in due:
        at["kf", 1] = at["kgs"]
    if "rx" in due:
        at["r"] = at["x%d" % place[0]] = at["rx"]
    col = moving(role[core])

    def after(q, deps):
        for d in deps:
            if seen.get((q, d[0]), 0) < d[1]:
                eng[q].wait_ge(T.sem[d[0]], d[1])
                seen[(q, d[0])] = d[1]

    banks = 7 if rank else 8
    users, turn, bank, own = [[] for _ in range(8)], [0], {}, {}
    B = range(4)

    def view(name, a, n):
        v = T[name][:, a:a + n]
        return v.bitcast(dt.uint8) if SCRATCH[name][2] == F8 else v

    def step(q, s):
        n = s[0]
        if q == "g":
            def transfers(k):
                for piece, ways, part, _ in s:
                    sem, parts = pieces(piece, role[core], role[core])
                    a, b, ca, _, w = parts[part][k]
                    for es, ds in ways:
                        sent[0] += len(es)
                        yield RemoteDMATransfer(
                            dst_ids=[DstId(rid=topo.addr(d)[0], pnc=topo.addr(d)[1]) for d in ds], dma_engine_mask=sum(1 << e for e in es),
                            remote_sem=T.sem[sem], srcs=[view(a, ca, w)], dsts=[view(b, pieces(piece, role[core], role[d])[1][part][k][3], w) for d in ds])

            def call():
                for k in range(len(pieces(s[0][0], role[core], role[core])[1][s[0][2]])):
                    g.remote_dma_fused(list(transfers(k)), local_sem=T.sem.sent)

            def needs(piece):
                sem, parts = pieces(piece, role[core], role[core])
                if piece[0][:2] in ("kc", "ks", "kk", "ta", "tb"):
                    return [d for a, _, ca, _, w in parts for b in range(ca // 128, (ca + w) // 128) for d in block[a, b]]
                if piece[0] == "a":
                    return [("Z", u) for u in range(piece[2], piece[3])]
                return {"rx": ["r", "x%d" % me], "kf": [("kf", 0)], "kg": [("kf", 0)], "oh": ["oh"], "kp": ["l_p" if rank else "kp"]}.get(piece[0], [sem])
            return [d for x in s for d in needs(x[0])], call, []
        if n == "Q":
            if s[1] == "k":
                a, e = 128 * int(s[2]), 128 * int(s[3])
                return ["l_" + s[1:3]], lambda: g.vector.quantize_mx(T.kc[:, a:e], T.ks[:, a:e], T.kt[:, 4 * a:4 * e]), [s[1:]]
            name, c, p, a, src = {"r": ("r", "mc", "mp", col[3], T.rtt[:]), "x": ("x%d" % me, "mc", "mp", col[2], T.xt[:]),
                                  "v": ("v%d" % keys, "vc", "vp", 128 * keys, T.vt[:])}[s[1:]]
            w = src.shape[1] // 4
            return ["l_" + s[1:]], lambda: g.vector.quantize_mx(T[c][:, a:a + w], T[p][:, a:a + w], src), [name]
        if n == "C":
            a = 32 * int(s[1])
            return ["l_q"], lambda: g.vector.tensor_copy(T.qpi[a:a + 32, 32:48], T.qld[0:32, :]), ["q%d" % me]
        if n == "h":
            b = int(s[1])
            a = 0 if b // 4 else 32
            return ([("kf", b // 4), "q%d" % place[a // 16]],
                    lambda: g.vector.tensor_scalar(T.og[:, 16 * b:16 * b + 16], T.qpi[:, a:a + 16], T.kf[:, b:b + 1], 255.0, SUB, MIN),
                    {3: ["og"], 7: ["oh"]}.get(b, []))
        if n == "F":
            a = int(s[1])
            return (["l_p" if rank and not a else "kp"], lambda: g.vector.tensor_scalar(T.kf[:, a:a + 4], T.kpi[:, a:a + 4], 128.0, None, SUB),
                    [("kf", a // 4)])
        if n == "l":
            (u0, u1), b = SPAN[s[1]], int(s[2])
            us = range(u0, u1)
            return ([("kf", b // 4)] + ["q%d" % place[u // 2] for u in us],
                    lambda: g.vector.tensor_scalar(T.of[:, 48 * b + 8 * u0:48 * b + 8 * u1], T.qpi[:, 8 * u0:8 * u1], T.kf[:, b:b + 1], 255.0, SUB, MIN),
                    [("of", b, u) for u in us])
        if n in "PS":
            b = int(s[-1])
            k = turn[0] % banks
            deps = block["kc", b] + block["ks", b] + users[k]
            if n == "P":
                deps, a, m, w, drains = deps + ["r"], 0, col[3], TQ, [("W", b)]
            else:
                us = range(*SPAN[s[1]])
                deps, a, m, w = deps + ["x%d" % place[u // 2] for u in us], U * us[0], col[us[0] // 2] + U * (us[0] % 2), U * len(us)
                drains = [("A", b, u) for u in us]

            def call():
                turn[0] += 1
                users[k] = drains
                for d in drains:
                    bank[d] = (k, a)
                return g.tensor.matmul_mx(T["ps%d" % k][:, 0:w], T.kc[:, 128 * b:128 * b + 128], T.ks[:, 128 * b:128 * b + 128],
                                          T.mc[:, m:m + w], T.mp[:, m:m + w], True, True)
            return deps, call, [("mm",) + d for d in drains]
        if n == "W":
            b = int(s[1])

            def call():
                d, p = T.pw[:, TQ * b:TQ * b + TQ], T["ps%d" % bank["W", b][0]][:, 0:TQ]
                return g.vector.tensor_copy(d, p) if q == "v" else g.scalar.activation(d, p, COPY)
            return [("mm", "W", b)], call, [("W", b)]
        if n == "Y":
            r, start, stop = s[1:]
            return (["v%d" % r] + [d for d in ("a%d" % r,) if d in due] + own.get(r, []),
                    lambda: g.tensor.matmul_mx(T.ps7[:, 0:TQ], T.vc[:, 128 * r:128 * r + 128], T.vp[:, 128 * r:128 * r + 128],
                                               T.ac[:, TQ * r:TQ * r + TQ], T.ap[:, TQ * r:TQ * r + TQ], start, stop), ["y"] if stop else [])
        if n == "O":
            return (["y"], lambda: g.vector.tensor_copy(T.ys[:], T.ps7[:, 0:TQ]) if q == "v" else g.scalar.activation(T.ys[:], T.ps7[:, 0:TQ], COPY),
                    ["out"])
        u0, u1 = SPAN[s[1]]
        us = range(u0, u1)
        b = int(s[2])
        h0 = 12 * TQ * (b // 4)
        if n == "Z":
            r = far[me] if b else keys
            c, p, a = ("ac", "ap", TQ * r + U * (u0 % 2)) if rank and u0 >= 4 else ("oc", "op", U * u0)
            w = U * (u1 - u0)
            return ([("R", e, u) for e in range(b, b + 4) for u in us],
                    lambda: g.vector.quantize_mx(T[c][:, a:a + w], T[p][:, a:a + w], T.ht[:, h0 + 4 * U * u0:h0 + 4 * U * u1]),
                    [("Z", u + 6 * (b // 4)) for u in us])
        if n == "G":
            given = b >= 4 and "og" in due
            li = T.og[:, 16 * (b - 6) + 8 * u0:16 * (b - 6) + 8 * u1] if given else T.of[:, 48 * b + 8 * u0:48 * b + 8 * u1]

            def call():
                o, w = T.gg[:, 768 * b + U * u0:768 * b + U * u1], T.pw[:, TQ * b:TQ * b + TQ].indirect(li)
                return g.vector.tensor_copy(o, w) if q == "v" else g.scalar.activation(o, w, COPY)
            return [("W", b)] + (["og"] if given else [("of", b, u) for u in us]), call, [("G", b, u) for u in us]
        if n == "A":

            def call():
                k, a = bank["A", b, u0]
                return g.vector.tensor_tensor(T.ht[:, h0 + 4 * U * u0 + b % 4:h0 + 4 * U * u1:4], T["ps%d" % k][:, U * u0 - a:U * u1 - a],
                                              T.gg[:, 768 * b + U * u0:768 * b + U * u1], ADD)
            return [("mm", "A", b, u) for u in us] + [("G", b, u) for u in us], call, [("A", b, u) for u in us]
        st = int(s[3])
        h = T.ht[:, h0 + 4 * U * u0 + b % 4:h0 + 4 * U * u1:st]
        part = [(c, u) for c in range(b, b // 4 * 4 + 4, st) for u in us]
        return ([("A",) + k for k in part],
                lambda: g.vector.tensor_scalar(h, h, 0.0, 0.03125, MAX, MULT) if q == "v" else g.scalar.activation(h, h, RELU, scale=0.03125),
                [("R",) + k for k in part])

    def run(queues):
        while any(queues.values()):
            moved = False
            for q, l in queues.items():
                while l:
                    deps, call, gives = step(q, l[0])
                    if not all(d in at for d in deps):
                        break
                    after(q, [at[d] for d in deps])
                    ins = call()
                    if q != "g":
                        ins.then_inc(T.sem[q + "s"], 1)
                        count[q] += 1
                        for k in gives:
                            at[k] = (q + "s", count[q])
                    l.pop(0)
                    moved = True
            assert moved, (core, queues)

    def cfg(q):
        out = []
        for s in CFG.get("%s%d.%s" % (kind, idx, q), CFG.get(kind + "." + q)).split():
            out += ["l%s%d" % (s[1], int(s[2]) + b) for b in B] if s[0] == "L" else ["h%d" % (b + 4 * (s == "J")) for b in B] if s in "HJ" else [s]
        return out

    queues = {q: cfg(q) for q in "vst"}
    queues["g"] = []
    for x in calls[core]:
        if x[3]:
            queues["g"][-1].append(x)
        else:
            queues["g"].append([x])
    if rank:
        for s in queues["v"]:
            if s[0] == "Z" and SPAN[s[1]][0] >= 4:
                own.setdefault(far[me] if int(s[2]) else keys, []).extend(("Z", u + 6 * (int(s[2]) // 4)) for u in range(*SPAN[s[1]]))
            if s[:2] == "Qk":
                for b in range(int(s[2]), int(s[3])):
                    block["kc", b] = block["ks", b] = [s[1:]]
        g.sync.dma_start(T.kpi[:, 0:4], T.kp[:]).then_inc(T.sem.l_p, 16)
        for k in range(2):
            g.scalar.dma_start(T.qld[16 * k:16 * k + 16, :], T.qp[:]).then_inc(T.sem.l_q, 16)
        src = {"r": (T.rtt[:], T.rt[:]), "x": (T.xt[:], T.qx[:]), "v": (T.vt[:], T.vv[:])}
        for n in CFG.get("loads%d" % me, CFG["loads"]).split():
            if n[0] == "~":
                after("y", [at["l_" + n[1:]]])
                continue
            if n[0] == "k":
                a, e = 512 * int(n[1]), 512 * int(n[2])
                src[n] = (T.kt[:, a:e], T.ky[:, a:e])
            g.sync.dma_start(*src[n]).then_inc(T.sem["l_" + n[:2]], 16)
            at["l_" + n[:2]] = ("l_" + n[:2], 16)
        at["l_q"], at["l_p"] = ("l_q", 32), ("l_p", 16)
        order = [(home if s[0] == "C" else far)[place["pni".index(s[1])]] for s in cfg("y")]
        ys = [("Y", r, r == order[0], r == order[-1]) for r in order]
        queues["t"] = [ys.pop(0) if s == "Y" else s for s in queues["t"]] + ys
        run(queues)
        last = "s" if at["out"][0] == "ss" else "y"
        after(last, [at["out"]])
        eng[last].dma_start(T.y[:], T.ys[:]).then_inc(T.sem.stored, 16)
        after("g", [("stored", 16)])
    else:
        run(queues)
    after("g", [(q + "s", count[q]) for q in count] + [("sent", sent[0])] + [(s, due[s]) for s in due])
